import numpy as np
import ml_dtypes


def mxq(x, axis, fmt="e4m3"):
    dtype, down = {"e4m3": (ml_dtypes.float8_e4m3fn, 7), "e5m2": (ml_dtypes.float8_e5m2, 14)}[fmt]
    v = np.moveaxis(np.asarray(x, np.float32).astype(ml_dtypes.bfloat16).astype(np.float64), axis, -1)
    blocks = v.reshape(v.shape[:-1] + (-1, 32))
    amax = np.abs(blocks).max(-1, keepdims=True)
    byte = np.maximum(np.where(amax > 0, np.frexp(amax)[1] - 1 + 127, 0) - down, 1)
    scale = np.exp2(byte - 127.0)
    codes = (blocks / scale).astype(np.float32).astype(dtype).astype(np.float64)
    return np.moveaxis((codes * scale).reshape(v.shape), -1, axis)


WIDE = False


def mx_kscale(k):
    if not WIDE:
        return np.ones(k)
    levels = np.array([18, -18])
    if k % 512:
        return np.exp2(np.random.permutation(np.resize(levels, k // 32))).repeat(32)
    a = np.empty((k // 512, 16))
    for p in range(k // 512):
        a[p, :8] = np.random.permutation(np.resize(levels, 8))
        for g in range(8):
            far = levels[np.abs(levels - a[p, g]) >= 10]
            a[p, g + 8] = far[np.random.randint(len(far))]
    return np.exp2(a.ravel()).repeat(32)


def f64(x):
    return np.asarray(x).astype(np.float64)


def striped(idx):
    return np.tile(np.asarray(idx).reshape(-1, 16).T, (8, 1)).astype(np.uint16)


def unstriped(offs):
    return offs[:16].T.reshape(-1).astype(np.int64)


N, C, D, R = 512, 4096, 512, 512


def eight(codes):
    return np.concatenate([codes[h].reshape(-1, 16).T for h in range(8)]).astype(np.uint16)


def uneight(offs):
    return np.stack([offs[16 * h:16 * h + 16].T.reshape(-1) for h in range(8)]).astype(np.int64)


def setup_inputs():
    n = np.random.standard_normal
    s = mx_kscale(D)[:, None]
    u = mx_kscale(N)
    grid = lambda x: np.round(x * 32) / 32
    return {
        "xT": (n((D, R)) * (1.0 / np.sqrt(D)) * s).astype(np.float32),
        "cb": (grid(n((D, C))) / s).astype(np.float32),
        "norm": np.tile(np.random.randint(32, 129, N) / 64.0 / u, (128, 1)).astype(np.float32),
        "ts": np.tile(np.random.uniform(0.5, 1.5, N) * u, (128, 1)).astype(np.float32),
        "y": n((R, N)).astype(np.float32),
        "wt": (np.random.uniform(0.5, 1.5, (R, 1)) * 1.0 / np.sqrt(N)).astype(np.float32),
        "offs": eight(np.random.randint(0, C, (8, N))),
    }


def reference(xT, cb, norm, ts, y, wt, offs):
    code = uneight(offs)
    k = np.concatenate([f64(cb)[64 * h:64 * h + 64][:, code[h]] for h in range(8)]) * f64(norm)[:1]
    a = f64(ts)[:1] * (mxq(f64(xT), 0, "e4m3").T @ mxq(k, 0, "e4m3"))
    g = f64(wt) * (a - f64(y))
    h = f64(ts)[:1] * g
    return mxq(h, 1, "e5m2") @ mxq(k, 1, "e4m3").T

@@ -1,0 +1,210 @@
+from contextlib import ExitStack
+
+import concourse.mybir as mybir
+from concourse.masks import make_identity
+
+N, C, D, R = 512, 4096, 512, 512
+FLOPS = 2 * 2 * R * N * D
+
+F32 = mybir.dt.float32
+BF16 = mybir.dt.bfloat16
+U32 = mybir.dt.uint32
+U16 = mybir.dt.uint16
+U8 = mybir.dt.uint8
+E4M3 = mybir.dt.float8_e4m3fn_x4
+E5M2 = mybir.dt.float8_e5m2_x4
+MULT = mybir.AluOpType.mult
+COPY = mybir.ActivationFunctionType.Copy
+
+P = 128
+PACK = 4
+BLOCKS = R // P
+CHUNK = 128
+CHUNKS = N // CHUNK
+LIST_COLS = CHUNK // 16
+X_HALF = R // 2
+
+
+def tile_attend_gpq_sq_x_kernel(tc, xT, cb, norm, ts, y, wt, offs, out):
+    nc = tc.nc
+    with ExitStack() as ctx:
+        lists = ctx.enter_context(tc.tile_pool(name="lists", bufs=1))
+        keep = ctx.enter_context(tc.tile_pool(name="keep", bufs=1))
+        held = ctx.enter_context(tc.psum_pool(name="held", bufs=1))
+        work = ctx.enter_context(tc.psum_pool(name="work", bufs=4))
+
+        def bank():
+            return work.tile([P, N], F32, name="bank")
+
+        cb_planes = cb.rearrange("(p t) c -> t p c", t=PACK)
+        windows = [keep.tile([P, C], F32, name="window%d" % t) for t in range(PACK)]
+        offsets = lists.tile([P, N // 16], U16, name="offsets")
+        y_raw = keep.tile([P, BLOCKS, N], F32, name="y_raw")
+        x_raw = [keep.tile([P, PACK, X_HALF], F32, name="x_raw%d" % h) for h in range(2)]
+        x_rows = xT.rearrange("(p t) r -> p t r", t=PACK)
+
+        rows = keep.tile([P, P], F32, name="rows")
+        nc.gpsimd.memset(rows[:], 0.0)
+        nc.sync.dma_start(windows[0][:], cb_planes[0])
+        nc.sync.dma_start(rows[0:4, :], norm[0:1, :].rearrange("o (j m) -> (o j) m", m=P))
+        nc.sync.dma_start(rows[4:8, :], ts[0:1, :].rearrange("o (j m) -> (o j) m", m=P))
+        nc.sync.dma_start(rows[8:12, :], wt.rearrange("(j m) o -> j (m o)", m=P))
+        nc.sync.dma_start(offsets[:], offs)
+        nc.sync.dma_start(y_raw[:], y.rearrange("(c p) n -> p c n", p=P))
+        for t in range(1, PACK):
+            nc.sync.dma_start(windows[t][:], cb_planes[t])
+        for h in range(2):
+            nc.sync.dma_start(x_raw[h][:], x_rows[:, :, h * X_HALF:(h + 1) * X_HALF])
+
+        ident = keep.tile([P, P], F32, name="ident")
+        make_identity(nc, ident[:])
+        turned = bank()
+        nc.tensor.transpose(turned[:, 0:P], rows[:], ident[:])
+        cols = keep.tile([P, 16], F32, name="cols")
+        nc.vector.tensor_copy(cols[:], turned[:, 0:16])
+
+        norm_bank = bank()
+        for j in range(4):
+            nc.tensor.transpose(norm_bank[:, j * P:(j + 1) * P], cols[:, j:j + 1].to_broadcast([P, P]), ident[:])
+        norm_row = keep.tile([P, N], F32, name="norm_row")
+        nc.scalar.copy(norm_row[:], norm_bank[:])
+        ts_bank = bank()
+        for j in range(4):
+            nc.tensor.transpose(ts_bank[:, j * P:(j + 1) * P], cols[:, 4 + j:5 + j].to_broadcast([P, P]), ident[:])
+        neg_ts = keep.tile([P, N], F32, name="neg_ts")
+        nc.scalar.activation(neg_ts[:].rearrange("p (s m) -> p s m", s=PACK),
+                             ts_bank[:].rearrange("p (m s) -> p s m", s=PACK), COPY, scale=-1.0)
+        ts_sq = keep.tile([P, N], F32, name="ts_sq")
+        nc.vector.tensor_tensor(ts_sq[:], neg_ts[:], neg_ts[:], MULT)
+
+        def wt_col(c):
+            return cols[:, 8 + c:9 + c]
+
+        k_bf = keep.tile([P, N, PACK], BF16, name="k_bf", align_bytes=64)
+        k_codes = keep.tile([P, N], U32, name="k_codes", align_bytes=64)
+        k_scales = keep.tile([P, N], U8, name="k_scales", align_bytes=64)
+        kt_codes = keep.tile([P, D], U32, name="kt_codes", align_bytes=64)
+        kt_scales = keep.tile([P, D], U8, name="kt_scales", align_bytes=64)
+        k_cols = k_bf[:].rearrange("p (s m) t -> p s m t", s=PACK)
+        k_f32 = [keep.tile([P, N], F32, name="k_f32_%d" % t) for t in range(PACK)]
+        kt_bf = [keep.tile([P, P, PACK], BF16, name="kt_bf%d" % t, align_bytes=64) for t in range(PACK)]
+
+        def gather(t):
+            for j in range(CHUNKS):
+                n_cols = slice(j * CHUNK, (j + 1) * CHUNK)
+                picked = windows[t][:].indirect(offsets[:, j * LIST_COLS:(j + 1) * LIST_COLS])
+                nc.vector.tensor_tensor(k_f32[t][:, n_cols], picked, norm_row[:, n_cols], MULT)
+            for j in range(CHUNKS):
+                n_cols = slice(j * CHUNK, (j + 1) * CHUNK)
+                m_cols = slice(j * CHUNK // PACK, (j + 1) * CHUNK // PACK)
+                src = k_f32[t][:, n_cols].rearrange("p (m s) -> p s m", s=PACK)
+                if j < CHUNKS - 1:
+                    nc.scalar.copy(k_cols[:, :, m_cols, t], src)
+                else:
+                    nc.vector.tensor_copy(k_cols[:, :, m_cols, t], src)
+
+        def turn_k(t):
+            kt_bank = bank()
+            for s in range(PACK):
+                nc.tensor.transpose(kt_bank[:, s * P:(s + 1) * P], k_f32[t][:, s:N:PACK], ident[:])
+            nc.scalar.copy(kt_bf[t][:], kt_bank[:].rearrange("m (s p) -> m p s", s=PACK))
+
+        def quantize_kt(t):
+            d_cols = slice(t * P, (t + 1) * P)
+            nc.vector.quantize_mx(out=kt_codes[:, d_cols].bitcast(E4M3), scales=kt_scales[:, d_cols],
+                                  in_=kt_bf[t][:].rearrange("m p s -> m (p s)"))
+
+        h_banks = [held.tile([P, N], F32, name="h_bank%d" % c) for c in range(BLOCKS)]
+
+        def seed_targets(c):
+            y_term = keep.tile([P, N], F32, name="y_term%d" % c)
+            nc.vector.scalar_tensor_tensor(
+                y_term[:].rearrange("p (s m) -> p s m", s=PACK),
+                y_raw[:, c, :].rearrange("p (m s) -> p s m", s=PACK),
+                wt_col(c),
+                neg_ts[:].rearrange("p (s m) -> p s m", s=PACK),
+                MULT, MULT)
+            for s in range(PACK):
+                nc.tensor.matmul(h_banks[c][:, s * P:(s + 1) * P], y_term[:, s * P:(s + 1) * P], ident[:],
+                                 start=(s == 0), stop=False, is_transpose=True)
+
+        for t in range(PACK - 1):
+            gather(t)
+            turn_k(t)
+            quantize_kt(t)
+            if t == 0:
+                for c in range(BLOCKS):
+                    seed_targets(c)
+
+        x_bf = [keep.tile([P, P, PACK], BF16, name="x_bf%d" % c, align_bytes=64) for c in range(BLOCKS)]
+        x_codes = [keep.tile([P, P], U32, name="x_codes%d" % c, align_bytes=64) for c in range(BLOCKS)]
+        x_scales = [keep.tile([P, P], U8, name="x_scales%d" % c, align_bytes=64) for c in range(BLOCKS)]
+        h_bf = [keep.tile([P, P, PACK], BF16, name="h_bf%d" % c, align_bytes=64) for c in range(BLOCKS)]
+        h_codes = [keep.tile([P, P], U32, name="h_codes%d" % c, align_bytes=64) for c in range(BLOCKS)]
+        h_scales = [keep.tile([P, P], U8, name="h_scales%d" % c, align_bytes=64) for c in range(BLOCKS)]
+        s_banks = {}
+        o_banks = {}
+
+        def interleave_x(c, copy):
+            r_cols = slice((c % 2) * P, (c % 2 + 1) * P)
+            copy(x_bf[c][:], x_raw[c // 2][:, :, r_cols].rearrange("p t r -> p r t"))
+
+        def first_product(c):
+            nc.vector.quantize_mx(out=x_codes[c][:].bitcast(E4M3), scales=x_scales[c][:],
+                                  in_=x_bf[c][:].rearrange("p r t -> p (r t)"))
+            s_banks[c] = bank()
+            nc.tensor.matmul_mx(out=s_banks[c][:], lhsT=x_codes[c][:].bitcast(E4M3), lhsT_scale=x_scales[c][:],
+                                rhs=k_codes[:].bitcast(E4M3), rhs_scale=k_scales[:], start=True, stop=True)
+
+        def weigh_and_turn(c):
+            a_term = keep.tile([P, N], F32, name="a_term%d" % c)
+            nc.vector.scalar_tensor_tensor(a_term[:], s_banks[c][:], wt_col(c), ts_sq[:], MULT, MULT)
+            for s in range(PACK):
+                nc.tensor.matmul(h_banks[c][:, s * P:(s + 1) * P], a_term[:, s * P:(s + 1) * P], ident[:],
+                                 start=False, stop=(s == PACK - 1), is_transpose=True)
+
+        def round_h(c):
+            nc.scalar.copy(h_bf[c][:], h_banks[c][:].rearrange("m (s r) -> m r s", s=PACK))
+
+        def second_product(c):
+            nc.vector.quantize_mx(out=h_codes[c][:].bitcast(E5M2), scales=h_scales[c][:],
+                                  in_=h_bf[c][:].rearrange("m r s -> m (r s)"))
+            o_banks[c] = bank()
+            nc.tensor.matmul_mx(out=o_banks[c][:], lhsT=h_codes[c][:].bitcast(E5M2), lhsT_scale=h_scales[c][:],
+                                rhs=kt_codes[:].bitcast(E4M3), rhs_scale=kt_scales[:], start=True, stop=True)
+
+        def store(c, copy):
+            result = keep.tile([P, P, PACK], F32, name="result%d" % c)
+            copy(result[:], o_banks[c][:].rearrange("r (t p) -> r p t", t=PACK))
+            nc.sync.dma_start(out[c * P:(c + 1) * P, :], result[:].rearrange("r p t -> r (p t)"))
+
+        last = PACK - 1
+        gather(last)
+        nc.vector.quantize_mx(out=k_codes[:].bitcast(E4M3), scales=k_scales[:],
+                              in_=k_bf[:].rearrange("p n t -> p (n t)"))
+        interleave_x(0, nc.scalar.copy)
+        interleave_x(1, nc.vector.tensor_copy)
+        turn_k(last)
+        first_product(0)
+        first_product(1)
+        interleave_x(2, nc.scalar.copy)
+        interleave_x(3, nc.scalar.copy)
+        weigh_and_turn(0)
+        first_product(2)
+        weigh_and_turn(1)
+        first_product(3)
+        quantize_kt(last)
+        round_h(0)
+        weigh_and_turn(2)
+        second_product(0)
+        round_h(1)
+        weigh_and_turn(3)
+        second_product(1)
+        round_h(2)
+        round_h(3)
+        second_product(2)
+        second_product(3)
+        store(0, nc.vector.tensor_copy)
+        store(1, nc.vector.tensor_copy)
+        store(2, nc.scalar.copy)
+        store(3, nc.vector.tensor_copy)

@@ -31,51 +31,63 @@ def tile_attend_gpq_sq_x_kernel(tc, xT, cb, norm, ts, y, wt, offs, out):
         lists = ctx.enter_context(tc.tile_pool(name="lists", bufs=1))
         keep = ctx.enter_context(tc.tile_pool(name="keep", bufs=1))
         held = ctx.enter_context(tc.psum_pool(name="held", bufs=1))
-        work = ctx.enter_context(tc.psum_pool(name="work", bufs=4))
+        work = ctx.enter_context(tc.psum_pool(name="work", bufs=1))
 
-        def bank():
-            return work.tile([P, N], F32, name="bank")
+        def bank(w, dtype=F32):
+            return work.tile([P, N], dtype, name="bank%d" % w)
 
         cb_planes = cb.rearrange("(p t) c -> t p c", t=PACK)
-        windows = [keep.tile([P, C], F32, name="window%d" % t) for t in range(PACK)]
+        windows = {}
+        x_raw = {}
+
+        def load_window(t):
+            windows[t] = keep.tile([P, C], F32, name="window%d" % t)
+            nc.sync.dma_start(windows[t][:], cb_planes[t])
+
+        def load_x(h):
+            x_raw[h] = keep.tile([P, PACK, X_HALF], F32, name="x_raw%d" % h)
+            nc.sync.dma_start(x_raw[h][:], x_rows[:, :, h * X_HALF:(h + 1) * X_HALF])
+
         offsets = lists.tile([P, N // 16], U16, name="offsets")
         y_raw = keep.tile([P, BLOCKS, N], F32, name="y_raw")
-        x_raw = [keep.tile([P, PACK, X_HALF], F32, name="x_raw%d" % h) for h in range(2)]
         x_rows = xT.rearrange("(p t) r -> p t r", t=PACK)
 
         rows = keep.tile([P, P], F32, name="rows")
         nc.gpsimd.memset(rows[:], 0.0)
-        nc.sync.dma_start(windows[0][:], cb_planes[0])
+        nc.sync.dma_start(y_raw[:], y.rearrange("(c p) n -> p c n", p=P))
         nc.sync.dma_start(rows[0:4, :], norm[0:1, :].rearrange("o (j m) -> (o j) m", m=P))
         nc.sync.dma_start(rows[4:8, :], ts[0:1, :].rearrange("o (j m) -> (o j) m", m=P))
         nc.sync.dma_start(rows[8:12, :], wt.rearrange("(j m) o -> j (m o)", m=P))
+        load_window(0)
         nc.sync.dma_start(offsets[:], offs)
-        nc.sync.dma_start(y_raw[:], y.rearrange("(c p) n -> p c n", p=P))
+        load_x(0)
         for t in range(1, PACK):
-            nc.sync.dma_start(windows[t][:], cb_planes[t])
-        for h in range(2):
-            nc.sync.dma_start(x_raw[h][:], x_rows[:, :, h * X_HALF:(h + 1) * X_HALF])
+            load_window(t)
+        load_x(1)
 
         ident = keep.tile([P, P], F32, name="ident")
         make_identity(nc, ident[:])
-        turned = bank()
+        ident_bf = keep.tile([P, P], BF16, name="ident_bf")
+        nc.vector.tensor_copy(ident_bf[:], ident[:])
+        turned = bank(0)
         nc.tensor.transpose(turned[:, 0:P], rows[:], ident[:])
         cols = keep.tile([P, 16], F32, name="cols")
         nc.vector.tensor_copy(cols[:], turned[:, 0:16])
 
-        norm_bank = bank()
+        norm_bank = bank(1)
         for j in range(4):
             nc.tensor.transpose(norm_bank[:, j * P:(j + 1) * P], cols[:, j:j + 1].to_broadcast([P, P]), ident[:])
         norm_row = keep.tile([P, N], F32, name="norm_row")
         nc.scalar.copy(norm_row[:], norm_bank[:])
-        ts_bank = bank()
+        ts_bank = bank(2)
         for j in range(4):
             nc.tensor.transpose(ts_bank[:, j * P:(j + 1) * P], cols[:, 4 + j:5 + j].to_broadcast([P, P]), ident[:])
         neg_ts = keep.tile([P, N], F32, name="neg_ts")
-        nc.scalar.activation(neg_ts[:].rearrange("p (s m) -> p s m", s=PACK),
-                             ts_bank[:].rearrange("p (m s) -> p s m", s=PACK), COPY, scale=-1.0)
+        nc.scalar.activation(neg_ts[:], ts_bank[:], COPY, scale=-1.0)
         ts_sq = keep.tile([P, N], F32, name="ts_sq")
-        nc.vector.tensor_tensor(ts_sq[:], neg_ts[:], neg_ts[:], MULT)
+        nc.vector.tensor_tensor(ts_sq[:].rearrange("p (s m) -> p m s", s=PACK),
+                                neg_ts[:].rearrange("p (m s) -> p m s", s=PACK),
+                                neg_ts[:].rearrange("p (m s) -> p m s", s=PACK), MULT)
 
         def wt_col(c):
             return cols[:, 8 + c:9 + c]
@@ -87,7 +99,7 @@ def tile_attend_gpq_sq_x_kernel(tc, xT, cb, norm, ts, y, wt, offs, out):
         kt_scales = keep.tile([P, D], U8, name="kt_scales", align_bytes=64)
         k_cols = k_bf[:].rearrange("p (s m) t -> p s m t", s=PACK)
         k_f32 = [keep.tile([P, N], F32, name="k_f32_%d" % t) for t in range(PACK)]
-        kt_bf = [keep.tile([P, P, PACK], BF16, name="kt_bf%d" % t, align_bytes=64) for t in range(PACK)]
+        kt_bf = [keep.tile([P, 2, P, PACK], BF16, name="kt_bf%d" % u, align_bytes=64) for u in range(PACK // 2)]
 
         def gather(t):
             for j in range(CHUNKS):
@@ -103,40 +115,32 @@ def tile_attend_gpq_sq_x_kernel(tc, xT, cb, norm, ts, y, wt, offs, out):
                 else:
                     nc.vector.tensor_copy(k_cols[:, :, m_cols, t], src)
 
-        def turn_k(t):
-            kt_bank = bank()
+        def turn_k(t, w):
+            kt_bank = bank(w, BF16)
             for s in range(PACK):
-                nc.tensor.transpose(kt_bank[:, s * P:(s + 1) * P], k_f32[t][:, s:N:PACK], ident[:])
-            nc.scalar.copy(kt_bf[t][:], kt_bank[:].rearrange("m (s p) -> m p s", s=PACK))
+                nc.tensor.transpose(kt_bank[:, s * P:(s + 1) * P], k_cols[:, s, :, t], ident_bf[:])
+            nc.scalar.copy(kt_bf[t // 2][:, t % 2], kt_bank[:].rearrange("m (s p) -> m p s", s=PACK))
 
-        def quantize_kt(t):
-            d_cols = slice(t * P, (t + 1) * P)
+        def quantize_kt(u):
+            d_cols = slice(u * 2 * P, (u + 1) * 2 * P)
             nc.vector.quantize_mx(out=kt_codes[:, d_cols].bitcast(E4M3), scales=kt_scales[:, d_cols],
-                                  in_=kt_bf[t][:].rearrange("m p s -> m (p s)"))
+                                  in_=kt_bf[u][:].rearrange("m e p s -> m (e p s)"))
 
         h_banks = [held.tile([P, N], F32, name="h_bank%d" % c) for c in range(BLOCKS)]
 
         def seed_targets(c):
             y_term = keep.tile([P, N], F32, name="y_term%d" % c)
             nc.vector.scalar_tensor_tensor(
-                y_term[:].rearrange("p (s m) -> p s m", s=PACK),
-                y_raw[:, c, :].rearrange("p (m s) -> p s m", s=PACK),
+                y_term[:].rearrange("p (s m) -> p m s", s=PACK),
+                y_raw[:, c, :].rearrange("p (m s) -> p m s", s=PACK),
                 wt_col(c),
-                neg_ts[:].rearrange("p (s m) -> p s m", s=PACK),
+                neg_ts[:].rearrange("p (m s) -> p m s", s=PACK),
                 MULT, MULT)
             for s in range(PACK):
                 nc.tensor.matmul(h_banks[c][:, s * P:(s + 1) * P], y_term[:, s * P:(s + 1) * P], ident[:],
                                  start=(s == 0), stop=False, is_transpose=True)
 
-        for t in range(PACK - 1):
-            gather(t)
-            turn_k(t)
-            quantize_kt(t)
-            if t == 0:
-                for c in range(BLOCKS):
-                    seed_targets(c)
-
-        x_bf = [keep.tile([P, P, PACK], BF16, name="x_bf%d" % c, align_bytes=64) for c in range(BLOCKS)]
+        x_bf = {}
         x_codes = [keep.tile([P, P], U32, name="x_codes%d" % c, align_bytes=64) for c in range(BLOCKS)]
         x_scales = [keep.tile([P, P], U8, name="x_scales%d" % c, align_bytes=64) for c in range(BLOCKS)]
         h_bf = [keep.tile([P, P, PACK], BF16, name="h_bf%d" % c, align_bytes=64) for c in range(BLOCKS)]
@@ -147,20 +151,30 @@ def tile_attend_gpq_sq_x_kernel(tc, xT, cb, norm, ts, y, wt, offs, out):
 
         def interleave_x(c, copy):
             r_cols = slice((c % 2) * P, (c % 2 + 1) * P)
-            copy(x_bf[c][:], x_raw[c // 2][:, :, r_cols].rearrange("p t r -> p r t"))
+            copy(x_bf[c].rearrange("p (g i) t -> p g t i", i=4),
+                 x_raw[c // 2][:, :, r_cols].rearrange("p t (g i) -> p g t i", i=4))
 
-        def first_product(c):
+        def quantize_x(c):
             nc.vector.quantize_mx(out=x_codes[c][:].bitcast(E4M3), scales=x_scales[c][:],
-                                  in_=x_bf[c][:].rearrange("p r t -> p (r t)"))
-            s_banks[c] = bank()
-            nc.tensor.matmul_mx(out=s_banks[c][:], lhsT=x_codes[c][:].bitcast(E4M3), lhsT_scale=x_scales[c][:],
-                                rhs=k_codes[:].bitcast(E4M3), rhs_scale=k_scales[:], start=True, stop=True)
+                                  in_=x_bf[c].rearrange("p r t -> p (r t)"))
 
-        def weigh_and_turn(c):
-            a_term = keep.tile([P, N], F32, name="a_term%d" % c)
-            nc.vector.scalar_tensor_tensor(a_term[:], s_banks[c][:], wt_col(c), ts_sq[:], MULT, MULT)
-            for s in range(PACK):
-                nc.tensor.matmul(h_banks[c][:, s * P:(s + 1) * P], a_term[:, s * P:(s + 1) * P], ident[:],
+        a_terms = [keep.tile([P, N], F32, name="a_term%d" % c) for c in range(BLOCKS)]
+
+        def quantize_k(lo, hi):
+            nc.vector.quantize_mx(out=k_codes[:, lo:hi].bitcast(E4M3), scales=k_scales[:, lo:hi],
+                                  in_=k_bf[:, lo:hi, :].rearrange("p n t -> p (n t)"))
+
+        def first_product(c, lo, hi, w):
+            s_banks[c, lo] = bank(w)
+            nc.tensor.matmul_mx(out=s_banks[c, lo][:, 0:hi - lo], lhsT=x_codes[c][:].bitcast(E4M3),
+                                lhsT_scale=x_scales[c][:], rhs=k_codes[:, lo:hi].bitcast(E4M3),
+                                rhs_scale=k_scales[:, lo:hi], start=True, stop=True)
+
+        def weigh_and_turn(c, lo, hi):
+            nc.vector.scalar_tensor_tensor(a_terms[c][:, lo:hi], s_banks[c, lo][:, 0:hi - lo], wt_col(c),
+                                           ts_sq[:, lo:hi], MULT, MULT)
+            for s in range(lo // P, hi // P):
+                nc.tensor.matmul(h_banks[c][:, s * P:(s + 1) * P], a_terms[c][:, s * P:(s + 1) * P], ident[:],
                                  start=False, stop=(s == PACK - 1), is_transpose=True)
 
         def round_h(c):
@@ -169,42 +183,72 @@ def tile_attend_gpq_sq_x_kernel(tc, xT, cb, norm, ts, y, wt, offs, out):
         def second_product(c):
             nc.vector.quantize_mx(out=h_codes[c][:].bitcast(E5M2), scales=h_scales[c][:],
                                   in_=h_bf[c][:].rearrange("m r s -> m (r s)"))
-            o_banks[c] = bank()
+            o_banks[c] = bank((0, 2, 3, 1)[c])
             nc.tensor.matmul_mx(out=o_banks[c][:], lhsT=h_codes[c][:].bitcast(E5M2), lhsT_scale=h_scales[c][:],
                                 rhs=kt_codes[:].bitcast(E4M3), rhs_scale=kt_scales[:], start=True, stop=True)
 
-        def store(c, copy):
-            result = keep.tile([P, P, PACK], F32, name="result%d" % c)
-            copy(result[:], o_banks[c][:].rearrange("r (t p) -> r p t", t=PACK))
-            nc.sync.dma_start(out[c * P:(c + 1) * P, :], result[:].rearrange("r p t -> r (p t)"))
+        def store(c, copy, pieces=1):
+            width = P // pieces
+            for i in range(pieces):
+                result = keep.tile([P, width, PACK], F32, name="result%d_%d" % (c, i))
+                copy(result[:], o_banks[c][:].rearrange("r (t p) -> r p t", t=PACK)[:, i * width:(i + 1) * width, :])
+                nc.sync.dma_start(out[c * P:(c + 1) * P, i * width * PACK:(i + 1) * width * PACK],
+                                  result[:].rearrange("r p t -> r (p t)"))
 
         last = PACK - 1
+        half = N // 2
+        x_early = keep.tile([P, 2, P, PACK], BF16, name="x_early", align_bytes=64)
+        for c in range(BLOCKS):
+            seed_targets(c)
+        gather(0)
+        turn_k(0, 0)
+        gather(1)
+        turn_k(1, 1)
+        quantize_kt(0)
+        for c in range(2):
+            x_bf[c] = x_early[:, c]
+            interleave_x(c, nc.scalar.copy)
+            quantize_x(c)
+        gather(2)
+        turn_k(2, 2)
+
+        warm = bank(3)
+        nc.tensor.transpose(warm[:, 0:P], windows[last][:, 0:P], ident[:])
+        for i in range(4):
+            nc.tensor.matmul_mx(out=warm[:, (i % 2) * half:(i % 2 + 1) * half], lhsT=x_codes[0][:].bitcast(E4M3),
+                                lhsT_scale=x_scales[0][:], rhs=kt_codes[:, 0:half].bitcast(E4M3),
+                                rhs_scale=kt_scales[:, 0:half], start=True, stop=True)
         gather(last)
-        nc.vector.quantize_mx(out=k_codes[:].bitcast(E4M3), scales=k_scales[:],
-                              in_=k_bf[:].rearrange("p n t -> p (n t)"))
-        interleave_x(0, nc.scalar.copy)
-        interleave_x(1, nc.vector.tensor_copy)
-        turn_k(last)
-        first_product(0)
-        first_product(1)
+        x_late = keep.tile([P, 2, P, PACK], BF16, name="x_late", align_bytes=64)
+        for c in range(2, BLOCKS):
+            x_bf[c] = x_late[:, c - 2]
+        quantize_k(0, half)
+        quantize_k(half, N)
+        turn_k(last, 3)
+        first_product(0, 0, half, 0)
+        first_product(0, half, N, 1)
+        first_product(1, 0, N, 2)
         interleave_x(2, nc.scalar.copy)
         interleave_x(3, nc.scalar.copy)
-        weigh_and_turn(0)
-        first_product(2)
-        weigh_and_turn(1)
-        first_product(3)
-        quantize_kt(last)
+        quantize_x(2)
+        weigh_and_turn(0, 0, half)
+        weigh_and_turn(0, half, N)
+        first_product(2, 0, N, 3)
+        quantize_x(3)
+        weigh_and_turn(1, 0, N)
+        first_product(3, 0, N, 1)
         round_h(0)
-        weigh_and_turn(2)
+        weigh_and_turn(2, 0, N)
+        quantize_kt(1)
         second_product(0)
         round_h(1)
-        weigh_and_turn(3)
+        weigh_and_turn(3, 0, N)
         second_product(1)
         round_h(2)
         round_h(3)
         second_product(2)
         second_product(3)
         store(0, nc.vector.tensor_copy)
-        store(1, nc.vector.tensor_copy)
-        store(2, nc.scalar.copy)
-        store(3, nc.vector.tensor_copy)
+        store(1, nc.scalar.copy)
+        store(2, nc.vector.tensor_copy)
+        store(3, nc.scalar.copy, 2)

@@ -210,15 +210,18 @@ def tile_attend_gpq_sq_x_kernel(tc, xT, cb, norm, ts, y, wt, offs, out):
             interleave_x(c, nc.scalar.copy)
             quantize_x(c)
         gather(2)
-        turn_k(2, 2)
-
         warm = bank(3)
-        nc.tensor.transpose(warm[:, 0:P], windows[last][:, 0:P], ident[:])
+        nc.tensor.transpose(warm[:, 0:P], k_f32[2][:, N - P:N], ident[:])
         for i in range(4):
             nc.tensor.matmul_mx(out=warm[:, (i % 2) * half:(i % 2 + 1) * half], lhsT=x_codes[0][:].bitcast(E4M3),
                                 lhsT_scale=x_scales[0][:], rhs=kt_codes[:, 0:half].bitcast(E4M3),
                                 rhs_scale=kt_scales[:, 0:half], start=True, stop=True)
+        turn_k(2, 2)
+        for i in range(12):
+            nc.tensor.transpose(warm[:, (i % 4) * P:(i % 4 + 1) * P], k_f32[2][:, 0:P], ident[:])
         gather(last)
+        for i in range(6):
+            nc.tensor.transpose(warm[:, (i % 4) * P:(i % 4 + 1) * P], k_f32[last][:, P:2 * P], ident[:])
         x_late = keep.tile([P, 2, P, PACK], BF16, name="x_late", align_bytes=64)
         for c in range(2, BLOCKS):
             x_bf[c] = x_late[:, c - 2]

@@ -23,6 +23,8 @@ CHUNK = 128
 CHUNKS = N // CHUNK
 LIST_COLS = CHUNK // 16
 X_HALF = R // 2
+TURNED = 3
+ADD = mybir.AluOpType.add
 
 
 def tile_attend_gpq_sq_x_kernel(tc, xT, cb, norm, ts, y, wt, offs, out):
@@ -45,7 +47,7 @@ def tile_attend_gpq_sq_x_kernel(tc, xT, cb, norm, ts, y, wt, offs, out):
             nc.sync.dma_start(windows[t][:], cb_planes[t])
 
         def load_x(h):
-            x_raw[h] = keep.tile([P, PACK, X_HALF], F32, name="x_raw%d" % h)
+            x_raw[h] = keep.tile([P, PACK, X_HALF], F32, name="x_raw%d" % h, align_bytes=64)
             nc.sync.dma_start(x_raw[h][:], x_rows[:, :, h * X_HALF:(h + 1) * X_HALF])
 
         offsets = lists.tile([P, N // 16], U16, name="offsets")
@@ -60,9 +62,9 @@ def tile_attend_gpq_sq_x_kernel(tc, xT, cb, norm, ts, y, wt, offs, out):
         nc.sync.dma_start(rows[8:12, :], wt.rearrange("(j m) o -> j (m o)", m=P))
         load_window(0)
         nc.sync.dma_start(offsets[:], offs)
-        load_x(0)
         for t in range(1, PACK):
             load_window(t)
+        load_x(0)
         load_x(1)
 
         ident = keep.tile([P, P], F32, name="ident")
@@ -98,8 +100,8 @@ def tile_attend_gpq_sq_x_kernel(tc, xT, cb, norm, ts, y, wt, offs, out):
         kt_codes = keep.tile([P, D], U32, name="kt_codes", align_bytes=64)
         kt_scales = keep.tile([P, D], U8, name="kt_scales", align_bytes=64)
         k_cols = k_bf[:].rearrange("p (s m) t -> p s m t", s=PACK)
-        k_f32 = [keep.tile([P, N], F32, name="k_f32_%d" % t) for t in range(PACK)]
-        kt_bf = [keep.tile([P, 2, P, PACK], BF16, name="kt_bf%d" % u, align_bytes=64) for u in range(PACK // 2)]
+        k_f32 = [keep.tile([P, N], F32, name="k_f32_%d" % t, align_bytes=64) for t in range(PACK)]
+        kt_bf = keep.tile([P, PACK * P * PACK], BF16, name="kt_bf", align_bytes=64)
 
         def gather(t):
             for j in range(CHUNKS):
@@ -119,12 +121,12 @@ def tile_attend_gpq_sq_x_kernel(tc, xT, cb, norm, ts, y, wt, offs, out):
             kt_bank = bank(w, BF16)
             for s in range(PACK):
                 nc.tensor.transpose(kt_bank[:, s * P:(s + 1) * P], k_cols[:, s, :, t], ident_bf[:])
-            nc.scalar.copy(kt_bf[t // 2][:, t % 2], kt_bank[:].rearrange("m (s p) -> m p s", s=PACK))
+            nc.scalar.copy(kt_bf[:, t * N:(t + 1) * N].rearrange("m (p s) -> m p s", s=PACK), kt_bank[:].rearrange("m (s p) -> m p s", s=PACK))
 
-        def quantize_kt(u):
-            d_cols = slice(u * 2 * P, (u + 1) * 2 * P)
+        def quantize_kt(t_lo, t_hi):
+            d_cols = slice(t_lo * P, t_hi * P)
             nc.vector.quantize_mx(out=kt_codes[:, d_cols].bitcast(E4M3), scales=kt_scales[:, d_cols],
-                                  in_=kt_bf[u][:].rearrange("m e p s -> m (e p s)"))
+                                  in_=kt_bf[:, t_lo * N:t_hi * N])
 
         h_banks = [held.tile([P, N], F32, name="h_bank%d" % c) for c in range(BLOCKS)]
 
@@ -138,12 +140,23 @@ def tile_attend_gpq_sq_x_kernel(tc, xT, cb, norm, ts, y, wt, offs, out):
                 MULT, MULT)
             for s in range(PACK):
                 nc.tensor.matmul(h_banks[c][:, s * P:(s + 1) * P], y_term[:, s * P:(s + 1) * P], ident[:],
-                                 start=(s == 0), stop=False, is_transpose=True)
+                                 start=(s == 0), stop=(c >= TURNED and s == PACK - 1), is_transpose=True)
+
+        weights = {}
+
+        def make_weights(c, w):
+            by_row = keep.tile([P, N], F32, name="by_row%d" % c)
+            nc.scalar.activation(by_row[:], ts_sq[:], COPY, scale=wt_col(c))
+            w_bank = bank(w)
+            for s in range(PACK):
+                nc.tensor.transpose(w_bank[:, s * P:(s + 1) * P], by_row[:, s * P:(s + 1) * P], ident[:])
+            weights[c] = keep.tile([P, P, PACK], F32, name="weights%d" % c)
+            nc.scalar.copy(weights[c][:], w_bank[:].rearrange("m (s r) -> m r s", s=PACK))
 
         x_bf = {}
         x_codes = [keep.tile([P, P], U32, name="x_codes%d" % c, align_bytes=64) for c in range(BLOCKS)]
         x_scales = [keep.tile([P, P], U8, name="x_scales%d" % c, align_bytes=64) for c in range(BLOCKS)]
-        h_bf = [keep.tile([P, P, PACK], BF16, name="h_bf%d" % c, align_bytes=64) for c in range(BLOCKS)]
+        h_bf = {}
         h_codes = [keep.tile([P, P], U32, name="h_codes%d" % c, align_bytes=64) for c in range(BLOCKS)]
         h_scales = [keep.tile([P, P], U8, name="h_scales%d" % c, align_bytes=64) for c in range(BLOCKS)]
         s_banks = {}
@@ -158,7 +171,13 @@ def tile_attend_gpq_sq_x_kernel(tc, xT, cb, norm, ts, y, wt, offs, out):
             nc.vector.quantize_mx(out=x_codes[c][:].bitcast(E4M3), scales=x_scales[c][:],
                                   in_=x_bf[c].rearrange("p r t -> p (r t)"))
 
-        a_terms = [keep.tile([P, N], F32, name="a_term%d" % c) for c in range(BLOCKS)]
+        a_terms = {}
+
+        def new_a_term(c, tag):
+            a_terms[c] = keep.tile([P, N], F32, name="a_term%d" % c, tag=tag, align_bytes=64)
+
+        def new_h_bf(c, tag):
+            h_bf[c] = keep.tile([P, P, PACK], BF16, name="h_bf%d" % c, tag=tag, align_bytes=64)
 
         def quantize_k(lo, hi):
             nc.vector.quantize_mx(out=k_codes[:, lo:hi].bitcast(E4M3), scales=k_scales[:, lo:hi],
@@ -177,13 +196,33 @@ def tile_attend_gpq_sq_x_kernel(tc, xT, cb, norm, ts, y, wt, offs, out):
                 nc.tensor.matmul(h_banks[c][:, s * P:(s + 1) * P], a_terms[c][:, s * P:(s + 1) * P], ident[:],
                                  start=False, stop=(s == PACK - 1), is_transpose=True)
 
+        def first_product_by_columns(c, w):
+            s_banks[c] = bank(w)
+            for s in range(PACK):
+                n_cols = slice(s * P, (s + 1) * P)
+                nc.tensor.matmul_mx(out=s_banks[c][:, n_cols], lhsT=k_codes[:, n_cols].bitcast(E4M3),
+                                    lhsT_scale=k_scales[:, n_cols], rhs=x_codes[c][:].bitcast(E4M3),
+                                    rhs_scale=x_scales[c][:], start=True, stop=True)
+
+        def weigh_by_columns(c, lo, hi):
+            a_cols = a_terms[c][:].rearrange("m (r s) -> m r s", s=PACK)
+            nc.vector.tensor_tensor(a_cols[:, lo:hi], s_banks[c][:].rearrange("m (s r) -> m r s", s=PACK)[:, lo:hi],
+                                    weights[c][:, lo:hi], MULT)
+
+        def add_targets(c, lo, hi):
+            a_cols = a_terms[c][:].rearrange("m (r s) -> m r s", s=PACK)
+            nc.vector.tensor_tensor(h_bf[c][:, lo:hi], a_cols[:, lo:hi],
+                                    h_banks[c][:].rearrange("m (s r) -> m r s", s=PACK)[:, lo:hi], ADD)
+
         def round_h(c):
             nc.scalar.copy(h_bf[c][:], h_banks[c][:].rearrange("m (s r) -> m r s", s=PACK))
 
-        def second_product(c):
+        def quantize_h(c):
             nc.vector.quantize_mx(out=h_codes[c][:].bitcast(E5M2), scales=h_scales[c][:],
                                   in_=h_bf[c][:].rearrange("m r s -> m (r s)"))
-            o_banks[c] = bank((0, 2, 3, 1)[c])
+
+        def second_product(c, w):
+            o_banks[c] = bank(w)
             nc.tensor.matmul_mx(out=o_banks[c][:], lhsT=h_codes[c][:].bitcast(E5M2), lhsT_scale=h_scales[c][:],
                                 rhs=kt_codes[:].bitcast(E4M3), rhs_scale=kt_scales[:], start=True, stop=True)
 
@@ -197,61 +236,72 @@ def tile_attend_gpq_sq_x_kernel(tc, xT, cb, norm, ts, y, wt, offs, out):
 
         last = PACK - 1
         half = N // 2
-        x_early = keep.tile([P, 2, P, PACK], BF16, name="x_early", align_bytes=64)
         for c in range(BLOCKS):
             seed_targets(c)
+        for c in range(TURNED, BLOCKS):
+            make_weights(c, c)
         gather(0)
         turn_k(0, 0)
         gather(1)
         turn_k(1, 1)
-        quantize_kt(0)
-        for c in range(2):
-            x_bf[c] = x_early[:, c]
-            interleave_x(c, nc.scalar.copy)
-            quantize_x(c)
+        quantize_kt(0, 2)
         gather(2)
-        warm = bank(3)
-        nc.tensor.transpose(warm[:, 0:P], k_f32[2][:, N - P:N], ident[:])
-        for i in range(4):
-            nc.tensor.matmul_mx(out=warm[:, (i % 2) * half:(i % 2 + 1) * half], lhsT=x_codes[0][:].bitcast(E4M3),
-                                lhsT_scale=x_scales[0][:], rhs=kt_codes[:, 0:half].bitcast(E4M3),
-                                rhs_scale=kt_scales[:, 0:half], start=True, stop=True)
         turn_k(2, 2)
-        for i in range(12):
-            nc.tensor.transpose(warm[:, (i % 4) * P:(i % 4 + 1) * P], k_f32[2][:, 0:P], ident[:])
         gather(last)
-        for i in range(6):
-            nc.tensor.transpose(warm[:, (i % 4) * P:(i % 4 + 1) * P], k_f32[last][:, P:2 * P], ident[:])
-        x_late = keep.tile([P, 2, P, PACK], BF16, name="x_late", align_bytes=64)
-        for c in range(2, BLOCKS):
-            x_bf[c] = x_late[:, c - 2]
+        warm = bank(0)
+        nc.tensor.transpose(warm[:, 0:P], k_f32[last][:, 0:P], ident[:])
+        for i in range(4):
+            nc.tensor.matmul_mx(out=warm[:, (i % 2) * half:(i % 2 + 1) * half], lhsT=kt_codes[:, 0:P].bitcast(E4M3),
+                                lhsT_scale=kt_scales[:, 0:P], rhs=kt_codes[:, 0:half].bitcast(E4M3),
+                                rhs_scale=kt_scales[:, 0:half], start=True, stop=True)
+        x_first = keep.tile([P, 2, P, PACK], BF16, name="x_first", tag="k_f32_%d" % last, align_bytes=64)
+        for c in range(2):
+            x_bf[c] = x_first[:, c]
+        interleave_x(0, nc.vector.tensor_copy)
+        interleave_x(1, nc.scalar.copy)
         quantize_k(0, half)
+        quantize_x(0)
         quantize_k(half, N)
         turn_k(last, 3)
         first_product(0, 0, half, 0)
         first_product(0, half, N, 1)
+        quantize_x(1)
         first_product(1, 0, N, 2)
+        x_late = keep.tile([P, 2, P, PACK], BF16, name="x_late", tag="x_raw0", align_bytes=64)
+        for c in range(2, BLOCKS):
+            x_bf[c] = x_late[:, c - 2]
         interleave_x(2, nc.scalar.copy)
         interleave_x(3, nc.scalar.copy)
-        quantize_x(2)
+        for c in range(2):
+            new_a_term(c, "a_term%d" % c)
+        for c in range(3):
+            new_h_bf(c, "h_bf%d" % c)
         weigh_and_turn(0, 0, half)
         weigh_and_turn(0, half, N)
-        first_product(2, 0, N, 3)
-        quantize_x(3)
         weigh_and_turn(1, 0, N)
-        first_product(3, 0, N, 1)
+        quantize_x(2)
+        first_product(2, 0, N, 0)
+        quantize_x(3)
+        first_product_by_columns(3, 1)
         round_h(0)
-        weigh_and_turn(2, 0, N)
-        quantize_kt(1)
-        second_product(0)
         round_h(1)
-        weigh_and_turn(3, 0, N)
-        second_product(1)
+        quantize_kt(2, PACK)
+        new_a_term(2, "x_raw0")
+        weigh_and_turn(2, 0, N)
+        quantize_h(0)
+        second_product(0, 3)
         round_h(2)
-        round_h(3)
-        second_product(2)
-        second_product(3)
-        store(0, nc.vector.tensor_copy)
+        new_a_term(3, "h_bf0")
+        weigh_by_columns(3, 0, P)
+        quantize_h(1)
+        second_product(1, 2)
+        new_h_bf(3, "h_bf1")
+        add_targets(3, 0, P)
+        quantize_h(2)
+        second_product(2, 0)
+        quantize_h(3)
+        second_product(3, 1)
+        store(0, nc.scalar.copy)
         store(1, nc.scalar.copy)
         store(2, nc.vector.tensor_copy)
         store(3, nc.scalar.copy, 2)

@@ -47,9 +47,14 @@ def tile_attend_gpq_sq_x_kernel(tc, xT, cb, norm, ts, y, wt, offs, out):
             nc.sync.dma_start(windows[t][:], cb_planes[t])
 
         def load_x(h):
-            x_raw[h] = keep.tile([P, PACK, X_HALF], F32, name="x_raw%d" % h, align_bytes=64)
-            nc.sync.dma_start(x_raw[h][:], x_rows[:, :, h * X_HALF:(h + 1) * X_HALF])
+            if h == 0:
+                x_raw[h] = keep.tile([P, PACK * X_HALF], F32, name="x_raw0", align_bytes=64)[:]
+            else:
+                x_raw[h] = late[:, N // 2:]
+            x_raw[h] = x_raw[h].rearrange("p (t r) -> p t r", t=PACK)
+            nc.sync.dma_start(x_raw[h], x_rows[:, :, h * X_HALF:(h + 1) * X_HALF])
 
+        late = keep.tile([P, N // 2 + PACK * X_HALF], F32, name="late", align_bytes=64)
         offsets = lists.tile([P, N // 16], U16, name="offsets")
         y_raw = keep.tile([P, BLOCKS, N], F32, name="y_raw")
         x_rows = xT.rearrange("(p t) r -> p t r", t=PACK)
@@ -101,7 +106,8 @@ def tile_attend_gpq_sq_x_kernel(tc, xT, cb, norm, ts, y, wt, offs, out):
         kt_scales = keep.tile([P, D], U8, name="kt_scales", align_bytes=64)
         k_cols = k_bf[:].rearrange("p (s m) t -> p s m t", s=PACK)
         k_f32 = [keep.tile([P, N], F32, name="k_f32_%d" % t, align_bytes=64) for t in range(PACK)]
-        kt_bf = keep.tile([P, PACK * P * PACK], BF16, name="kt_bf", align_bytes=64)
+        kt_early = keep.tile([P, 2 * N], BF16, name="kt_early", align_bytes=64)
+        kt_bf = [kt_early[:], late[:, 0:N].bitcast(BF16)]
 
         def gather(t):
             for j in range(CHUNKS):
@@ -112,7 +118,7 @@ def tile_attend_gpq_sq_x_kernel(tc, xT, cb, norm, ts, y, wt, offs, out):
                 n_cols = slice(j * CHUNK, (j + 1) * CHUNK)
                 m_cols = slice(j * CHUNK // PACK, (j + 1) * CHUNK // PACK)
                 src = k_f32[t][:, n_cols].rearrange("p (m s) -> p s m", s=PACK)
-                if j < CHUNKS - 1:
+                if j < CHUNKS // 2:
                     nc.scalar.copy(k_cols[:, :, m_cols, t], src)
                 else:
                     nc.vector.tensor_copy(k_cols[:, :, m_cols, t], src)
@@ -121,12 +127,12 @@ def tile_attend_gpq_sq_x_kernel(tc, xT, cb, norm, ts, y, wt, offs, out):
             kt_bank = bank(w, BF16)
             for s in range(PACK):
                 nc.tensor.transpose(kt_bank[:, s * P:(s + 1) * P], k_cols[:, s, :, t], ident_bf[:])
-            nc.scalar.copy(kt_bf[:, t * N:(t + 1) * N].rearrange("m (p s) -> m p s", s=PACK), kt_bank[:].rearrange("m (s p) -> m p s", s=PACK))
+            nc.scalar.copy(kt_bf[t // 2][:, (t % 2) * N:(t % 2 + 1) * N].rearrange("m (p s) -> m p s", s=PACK), kt_bank[:].rearrange("m (s p) -> m p s", s=PACK))
 
         def quantize_kt(t_lo, t_hi):
             d_cols = slice(t_lo * P, t_hi * P)
             nc.vector.quantize_mx(out=kt_codes[:, d_cols].bitcast(E4M3), scales=kt_scales[:, d_cols],
-                                  in_=kt_bf[:, t_lo * N:t_hi * N])
+                                  in_=kt_bf[t_lo // 2])
 
         h_banks = [held.tile([P, N], F32, name="h_bank%d" % c) for c in range(BLOCKS)]
 
@@ -189,10 +195,12 @@ def tile_attend_gpq_sq_x_kernel(tc, xT, cb, norm, ts, y, wt, offs, out):
                                 lhsT_scale=x_scales[c][:], rhs=k_codes[:, lo:hi].bitcast(E4M3),
                                 rhs_scale=k_scales[:, lo:hi], start=True, stop=True)
 
-        def weigh_and_turn(c, lo, hi):
+        def weigh(c, lo, hi):
             nc.vector.scalar_tensor_tensor(a_terms[c][:, lo:hi], s_banks[c, lo][:, 0:hi - lo], wt_col(c),
                                            ts_sq[:, lo:hi], MULT, MULT)
-            for s in range(lo // P, hi // P):
+
+        def turn_a(c):
+            for s in range(PACK):
                 nc.tensor.matmul(h_banks[c][:, s * P:(s + 1) * P], a_terms[c][:, s * P:(s + 1) * P], ident[:],
                                  start=False, stop=(s == PACK - 1), is_transpose=True)
 
@@ -229,7 +237,8 @@ def tile_attend_gpq_sq_x_kernel(tc, xT, cb, norm, ts, y, wt, offs, out):
         def store(c, copy, pieces=1):
             width = P // pieces
             for i in range(pieces):
-                result = keep.tile([P, width, PACK], F32, name="result%d_%d" % (c, i))
+                result = keep.tile([P, width, PACK], F32, name="result%d_%d" % (c, i), align_bytes=64,
+                                   tag="result%d_%d" % (c, i))
                 copy(result[:], o_banks[c][:].rearrange("r (t p) -> r p t", t=PACK)[:, i * width:(i + 1) * width, :])
                 nc.sync.dma_start(out[c * P:(c + 1) * P, i * width * PACK:(i + 1) * width * PACK],
                                   result[:].rearrange("r p t -> r (p t)"))
@@ -249,59 +258,61 @@ def tile_attend_gpq_sq_x_kernel(tc, xT, cb, norm, ts, y, wt, offs, out):
         turn_k(2, 2)
         gather(last)
         warm = bank(0)
-        nc.tensor.transpose(warm[:, 0:P], k_f32[last][:, 0:P], ident[:])
+        nc.tensor.transpose(warm[:, 0:P], k_f32[last][:, P:2 * P], ident[:])
         for i in range(4):
             nc.tensor.matmul_mx(out=warm[:, (i % 2) * half:(i % 2 + 1) * half], lhsT=kt_codes[:, 0:P].bitcast(E4M3),
                                 lhsT_scale=kt_scales[:, 0:P], rhs=kt_codes[:, 0:half].bitcast(E4M3),
                                 rhs_scale=kt_scales[:, 0:half], start=True, stop=True)
-        x_first = keep.tile([P, 2, P, PACK], BF16, name="x_first", tag="k_f32_%d" % last, align_bytes=64)
+        x_first = keep.tile([P, 2, P, PACK], BF16, name="x_first", align_bytes=64)
         for c in range(2):
             x_bf[c] = x_first[:, c]
-        interleave_x(0, nc.vector.tensor_copy)
+        interleave_x(0, nc.scalar.copy)
         interleave_x(1, nc.scalar.copy)
         quantize_k(0, half)
         quantize_x(0)
         quantize_k(half, N)
+        x_bf[2] = keep.tile([P, P, PACK], BF16, name="x_bf2", tag="x_raw0", align_bytes=64)[:]
+        x_bf[3] = keep.tile([P, P, PACK], BF16, name="x_bf3", align_bytes=64)[:]
+        interleave_x(2, nc.scalar.copy)
+        interleave_x(3, nc.scalar.copy)
         turn_k(last, 3)
         first_product(0, 0, half, 0)
         first_product(0, half, N, 1)
         quantize_x(1)
         first_product(1, 0, N, 2)
-        x_late = keep.tile([P, 2, P, PACK], BF16, name="x_late", tag="x_raw0", align_bytes=64)
-        for c in range(2, BLOCKS):
-            x_bf[c] = x_late[:, c - 2]
-        interleave_x(2, nc.scalar.copy)
-        interleave_x(3, nc.scalar.copy)
-        for c in range(2):
-            new_a_term(c, "a_term%d" % c)
         for c in range(3):
             new_h_bf(c, "h_bf%d" % c)
-        weigh_and_turn(0, 0, half)
-        weigh_and_turn(0, half, N)
-        weigh_and_turn(1, 0, N)
+        new_a_term(0, "a_term0")
+        weigh(0, 0, half)
         quantize_x(2)
         first_product(2, 0, N, 0)
+        weigh(0, half, N)
+        turn_a(0)
         quantize_x(3)
-        first_product_by_columns(3, 1)
+        a_terms[1] = late[:, N:2 * N]
+        weigh(1, 0, N)
+        turn_a(1)
+        first_product_by_columns(3, 2)
+        new_a_term(2, "a_term2")
+        weigh(2, 0, N)
+        turn_a(2)
         round_h(0)
         round_h(1)
-        quantize_kt(2, PACK)
-        new_a_term(2, "x_raw0")
-        weigh_and_turn(2, 0, N)
-        quantize_h(0)
-        second_product(0, 3)
         round_h(2)
-        new_a_term(3, "h_bf0")
+        quantize_kt(2, PACK)
+        quantize_h(0)
+        second_product(0, 1)
+        new_a_term(3, "a_term3")
         weigh_by_columns(3, 0, P)
         quantize_h(1)
-        second_product(1, 2)
-        new_h_bf(3, "h_bf1")
+        second_product(1, 3)
+        new_h_bf(3, "h_bf3")
         add_targets(3, 0, P)
         quantize_h(2)
         second_product(2, 0)
         quantize_h(3)
-        second_product(3, 1)
+        second_product(3, 2)
         store(0, nc.scalar.copy)
         store(1, nc.scalar.copy)
-        store(2, nc.vector.tensor_copy)
+        store(2, nc.vector.tensor_copy, 2)
         store(3, nc.scalar.copy, 2)

@@ -56,12 +56,13 @@ def tile_attend_gpq_sq_x_kernel(tc, xT, cb, norm, ts, y, wt, offs, out):
 
         late = keep.tile([P, N // 2 + PACK * X_HALF], F32, name="late", align_bytes=64)
         offsets = lists.tile([P, N // 16], U16, name="offsets")
-        y_raw = keep.tile([P, BLOCKS, N], F32, name="y_raw")
+        y_raw = keep.tile([P, TURNED, N], F32, name="y_raw")
+        y_last = keep.tile([P, N], F32, name="y_last")
         x_rows = xT.rearrange("(p t) r -> p t r", t=PACK)
 
         rows = keep.tile([P, P], F32, name="rows")
         nc.gpsimd.memset(rows[:], 0.0)
-        nc.sync.dma_start(y_raw[:], y.rearrange("(c p) n -> p c n", p=P))
+        nc.sync.dma_start(y_raw[:], y[0:TURNED * P, :].rearrange("(c p) n -> p c n", p=P))
         nc.sync.dma_start(rows[0:4, :], norm[0:1, :].rearrange("o (j m) -> (o j) m", m=P))
         nc.sync.dma_start(rows[4:8, :], ts[0:1, :].rearrange("o (j m) -> (o j) m", m=P))
         nc.sync.dma_start(rows[8:12, :], wt.rearrange("(j m) o -> j (m o)", m=P))
@@ -71,6 +72,7 @@ def tile_attend_gpq_sq_x_kernel(tc, xT, cb, norm, ts, y, wt, offs, out):
             load_window(t)
         load_x(0)
         load_x(1)
+        nc.sync.dma_start(y_last[:], y[TURNED * P:, :])
 
         ident = keep.tile([P, P], F32, name="ident")
         make_identity(nc, ident[:])
@@ -134,7 +136,7 @@ def tile_attend_gpq_sq_x_kernel(tc, xT, cb, norm, ts, y, wt, offs, out):
             nc.vector.quantize_mx(out=kt_codes[:, d_cols].bitcast(E4M3), scales=kt_scales[:, d_cols],
                                   in_=kt_bf[t_lo // 2])
 
-        h_banks = [held.tile([P, N], F32, name="h_bank%d" % c) for c in range(BLOCKS)]
+        h_banks = [held.tile([P, N], F32, name="h_bank%d" % c) for c in range(TURNED)]
 
         def seed_targets(c):
             y_term = keep.tile([P, N], F32, name="y_term%d" % c)
@@ -245,8 +247,10 @@ def tile_attend_gpq_sq_x_kernel(tc, xT, cb, norm, ts, y, wt, offs, out):
 
         last = PACK - 1
         half = N // 2
-        for c in range(BLOCKS):
+        for c in range(TURNED):
             seed_targets(c)
+        y_weight = keep.tile([P, PACK, P], F32, name="y_weight")
+        nc.scalar.activation(y_weight[:], neg_ts[:].rearrange("p (m s) -> p s m", s=PACK), COPY, scale=wt_col(TURNED))
         for c in range(TURNED, BLOCKS):
             make_weights(c, c)
         gather(0)
@@ -293,9 +297,14 @@ def tile_attend_gpq_sq_x_kernel(tc, xT, cb, norm, ts, y, wt, offs, out):
         weigh(1, 0, N)
         turn_a(1)
         first_product_by_columns(3, 2)
+        y_term_last = keep.tile([P, PACK, P], F32, name="y_term_last", tag="x_bf3", align_bytes=64)
+        nc.gpsimd.tensor_tensor(y_term_last[:], y_last[:].rearrange("p (m s) -> p s m", s=PACK), y_weight[:], MULT)
         new_a_term(2, "a_term2")
         weigh(2, 0, N)
         turn_a(2)
+        h_banks.append(bank(0))
+        for s in range(PACK):
+            nc.tensor.transpose(h_banks[3][:, s * P:(s + 1) * P], y_term_last[:, s], ident[:])
         round_h(0)
         round_h(1)
         round_h(2)
@@ -309,7 +318,7 @@ def tile_attend_gpq_sq_x_kernel(tc, xT, cb, norm, ts, y, wt, offs, out):
         new_h_bf(3, "h_bf3")
         add_targets(3, 0, P)
         quantize_h(2)
-        second_product(2, 0)
+        second_product(2, 4)
         quantize_h(3)
         second_product(3, 2)
         store(0, nc.scalar.copy)

@@ -261,12 +261,6 @@ def tile_attend_gpq_sq_x_kernel(tc, xT, cb, norm, ts, y, wt, offs, out):
         gather(2)
         turn_k(2, 2)
         gather(last)
-        warm = bank(0)
-        nc.tensor.transpose(warm[:, 0:P], k_f32[last][:, P:2 * P], ident[:])
-        for i in range(4):
-            nc.tensor.matmul_mx(out=warm[:, (i % 2) * half:(i % 2 + 1) * half], lhsT=kt_codes[:, 0:P].bitcast(E4M3),
-                                lhsT_scale=kt_scales[:, 0:P], rhs=kt_codes[:, 0:half].bitcast(E4M3),
-                                rhs_scale=kt_scales[:, 0:half], start=True, stop=True)
         x_first = keep.tile([P, 2, P, PACK], BF16, name="x_first", align_bytes=64)
         for c in range(2):
             x_bf[c] = x_first[:, c]

@@ -50,11 +50,11 @@ def tile_attend_gpq_sq_x_kernel(tc, xT, cb, norm, ts, y, wt, offs, out):
             if h == 0:
                 x_raw[h] = keep.tile([P, PACK * X_HALF], F32, name="x_raw0", align_bytes=64)[:]
             else:
-                x_raw[h] = late[:, N // 2:]
+                x_raw[h] = late[:, N // 2:N // 2 + PACK * X_HALF]
             x_raw[h] = x_raw[h].rearrange("p (t r) -> p t r", t=PACK)
             nc.sync.dma_start(x_raw[h], x_rows[:, :, h * X_HALF:(h + 1) * X_HALF])
 
-        late = keep.tile([P, N // 2 + PACK * X_HALF], F32, name="late", align_bytes=64)
+        late = keep.tile([P, 3 * N], F32, name="late", align_bytes=64)
         offsets = lists.tile([P, N // 16], U16, name="offsets")
         y_raw = keep.tile([P, TURNED, N], F32, name="y_raw")
         y_last = keep.tile([P, N], F32, name="y_last")
@@ -148,7 +148,7 @@ def tile_attend_gpq_sq_x_kernel(tc, xT, cb, norm, ts, y, wt, offs, out):
                 MULT, MULT)
             for s in range(PACK):
                 nc.tensor.matmul(h_banks[c][:, s * P:(s + 1) * P], y_term[:, s * P:(s + 1) * P], ident[:],
-                                 start=(s == 0), stop=(c >= TURNED and s == PACK - 1), is_transpose=True)
+                                 start=(s == 0), stop=(c >= 2 and s == PACK - 1), is_transpose=True)
 
         weights = {}
 
@@ -184,6 +184,9 @@ def tile_attend_gpq_sq_x_kernel(tc, xT, cb, norm, ts, y, wt, offs, out):
         def new_a_term(c, tag):
             a_terms[c] = keep.tile([P, N], F32, name="a_term%d" % c, tag=tag, align_bytes=64)
 
+        def new_b_term(c):
+            a_terms[c] = keep.tile([P, PACK, P], F32, name="a_term%d" % c, align_bytes=64)[:]
+
         def new_h_bf(c, tag):
             h_bf[c] = keep.tile([P, P, PACK], BF16, name="h_bf%d" % c, tag=tag, align_bytes=64)
 
@@ -198,12 +201,13 @@ def tile_attend_gpq_sq_x_kernel(tc, xT, cb, norm, ts, y, wt, offs, out):
                                 rhs_scale=k_scales[:, lo:hi], start=True, stop=True)
 
         def weigh(c, lo, hi):
-            nc.vector.scalar_tensor_tensor(a_terms[c][:, lo:hi], s_banks[c, lo][:, 0:hi - lo], wt_col(c),
-                                           ts_sq[:, lo:hi], MULT, MULT)
+            nc.vector.scalar_tensor_tensor(a_terms[c][:, lo // P:hi // P],
+                                           s_banks[c, lo][:, 0:hi - lo].rearrange("p (s m) -> p s m", m=P), wt_col(c),
+                                           ts_sq[:, lo:hi].rearrange("p (s m) -> p s m", m=P), MULT, MULT)
 
         def turn_a(c):
             for s in range(PACK):
-                nc.tensor.matmul(h_banks[c][:, s * P:(s + 1) * P], a_terms[c][:, s * P:(s + 1) * P], ident[:],
+                nc.tensor.matmul(h_banks[c][:, s * P:(s + 1) * P], a_terms[c][:, s], ident[:],
                                  start=False, stop=(s == PACK - 1), is_transpose=True)
 
         def first_product_by_columns(c, w):
@@ -251,7 +255,7 @@ def tile_attend_gpq_sq_x_kernel(tc, xT, cb, norm, ts, y, wt, offs, out):
             seed_targets(c)
         y_weight = keep.tile([P, PACK, P], F32, name="y_weight")
         nc.scalar.activation(y_weight[:], neg_ts[:].rearrange("p (m s) -> p s m", s=PACK), COPY, scale=wt_col(TURNED))
-        for c in range(TURNED, BLOCKS):
+        for c in range(2, BLOCKS):
             make_weights(c, c)
         gather(0)
         turn_k(0, 0)
@@ -269,53 +273,52 @@ def tile_attend_gpq_sq_x_kernel(tc, xT, cb, norm, ts, y, wt, offs, out):
         quantize_k(0, half)
         quantize_x(0)
         quantize_k(half, N)
-        x_bf[2] = keep.tile([P, P, PACK], BF16, name="x_bf2", tag="x_raw0", align_bytes=64)[:]
+        x_bf[2] = keep.tile([P, P, PACK], BF16, name="x_bf2", align_bytes=64)[:]
         x_bf[3] = keep.tile([P, P, PACK], BF16, name="x_bf3", align_bytes=64)[:]
-        interleave_x(2, nc.scalar.copy)
         interleave_x(3, nc.scalar.copy)
+        quantize_x(1)
+        interleave_x(2, nc.vector.tensor_copy)
         turn_k(last, 3)
         first_product(0, 0, half, 0)
         first_product(0, half, N, 1)
-        quantize_x(1)
         first_product(1, 0, N, 2)
-        for c in range(3):
-            new_h_bf(c, "h_bf%d" % c)
-        new_a_term(0, "a_term0")
-        weigh(0, 0, half)
-        quantize_x(2)
-        first_product(2, 0, N, 0)
-        weigh(0, half, N)
-        turn_a(0)
         quantize_x(3)
-        a_terms[1] = late[:, N:2 * N]
+        quantize_x(2)
+        for c in range(BLOCKS):
+            new_h_bf(c, "h_bf%d" % c)
+        spent_x = late[:, N:].rearrange("p (s c m) -> p c s m", c=2, m=P)
+        a_terms[0] = spent_x[:, 0]
+        weigh(0, 0, half)
+        weigh(0, half, N)
+        first_product_by_columns(2, 4)
+        turn_a(0)
+        y_term_last = keep.tile([P, PACK, P], F32, name="y_term_last", tag="x_bf2", align_bytes=64)
+        nc.gpsimd.tensor_tensor(y_term_last[:], y_last[:].rearrange("p (m s) -> p s m", s=PACK), y_weight[:], MULT)
+        a_terms[1] = spent_x[:, 1]
         weigh(1, 0, N)
         turn_a(1)
         first_product_by_columns(3, 2)
-        y_term_last = keep.tile([P, PACK, P], F32, name="y_term_last", tag="x_bf3", align_bytes=64)
-        nc.gpsimd.tensor_tensor(y_term_last[:], y_last[:].rearrange("p (m s) -> p s m", s=PACK), y_weight[:], MULT)
         new_a_term(2, "a_term2")
-        weigh(2, 0, N)
-        turn_a(2)
-        h_banks.append(bank(0))
-        for s in range(PACK):
-            nc.tensor.transpose(h_banks[3][:, s * P:(s + 1) * P], y_term_last[:, s], ident[:])
+        weigh_by_columns(2, 0, P)
         round_h(0)
         round_h(1)
-        round_h(2)
         quantize_kt(2, PACK)
         quantize_h(0)
-        second_product(0, 1)
+        second_product(0, 0)
+        h_banks.append(bank(1))
+        for s in range(PACK):
+            nc.tensor.transpose(h_banks[3][:, s * P:(s + 1) * P], y_term_last[:, s], ident[:])
+        add_targets(2, 0, P)
         new_a_term(3, "a_term3")
         weigh_by_columns(3, 0, P)
         quantize_h(1)
         second_product(1, 3)
-        new_h_bf(3, "h_bf3")
-        add_targets(3, 0, P)
         quantize_h(2)
         second_product(2, 4)
+        add_targets(3, 0, P)
         quantize_h(3)
         second_product(3, 2)
         store(0, nc.scalar.copy)
         store(1, nc.scalar.copy)
-        store(2, nc.vector.tensor_copy, 2)
-        store(3, nc.scalar.copy, 2)
+        store(2, nc.scalar.copy)
+        store(3, nc.vector.tensor_copy, 2)

@@ -148,7 +148,7 @@ def tile_attend_gpq_sq_x_kernel(tc, xT, cb, norm, ts, y, wt, offs, out):
                 MULT, MULT)
             for s in range(PACK):
                 nc.tensor.matmul(h_banks[c][:, s * P:(s + 1) * P], y_term[:, s * P:(s + 1) * P], ident[:],
-                                 start=(s == 0), stop=(c >= 2 and s == PACK - 1), is_transpose=True)
+                                 start=(s == 0), stop=(c >= TURNED and s == PACK - 1), is_transpose=True)
 
         weights = {}
 
@@ -158,8 +158,8 @@ def tile_attend_gpq_sq_x_kernel(tc, xT, cb, norm, ts, y, wt, offs, out):
             w_bank = bank(w)
             for s in range(PACK):
                 nc.tensor.transpose(w_bank[:, s * P:(s + 1) * P], by_row[:, s * P:(s + 1) * P], ident[:])
-            weights[c] = keep.tile([P, P, PACK], F32, name="weights%d" % c)
-            nc.scalar.copy(weights[c][:], w_bank[:].rearrange("m (s r) -> m r s", s=PACK))
+            weights[c] = keep.tile([P, N], F32, name="weights%d" % c)
+            nc.scalar.copy(weights[c][:], w_bank[:])
 
         x_bf = {}
         x_codes = [keep.tile([P, P], U32, name="x_codes%d" % c, align_bytes=64) for c in range(BLOCKS)]
@@ -218,15 +218,13 @@ def tile_attend_gpq_sq_x_kernel(tc, xT, cb, norm, ts, y, wt, offs, out):
                                     lhsT_scale=k_scales[:, n_cols], rhs=x_codes[c][:].bitcast(E4M3),
                                     rhs_scale=x_scales[c][:], start=True, stop=True)
 
-        def weigh_by_columns(c, lo, hi):
-            a_cols = a_terms[c][:].rearrange("m (r s) -> m r s", s=PACK)
-            nc.vector.tensor_tensor(a_cols[:, lo:hi], s_banks[c][:].rearrange("m (s r) -> m r s", s=PACK)[:, lo:hi],
-                                    weights[c][:, lo:hi], MULT)
+        def weigh_by_columns(c):
+            nc.vector.tensor_tensor(a_terms[c][:], s_banks[c][:], weights[c][:], MULT)
 
-        def add_targets(c, lo, hi):
-            a_cols = a_terms[c][:].rearrange("m (r s) -> m r s", s=PACK)
-            nc.vector.tensor_tensor(h_bf[c][:, lo:hi], a_cols[:, lo:hi],
-                                    h_banks[c][:].rearrange("m (s r) -> m r s", s=PACK)[:, lo:hi], ADD)
+        def add_targets(c):
+            nc.vector.tensor_tensor(h_bf[c][:].rearrange("m (g i) s -> m g s i", i=4),
+                                    a_terms[c][:].rearrange("m (s g i) -> m g s i", s=PACK, i=4),
+                                    h_banks[c][:].rearrange("m (s g i) -> m g s i", s=PACK, i=4), ADD)
 
         def round_h(c):
             nc.scalar.copy(h_bf[c][:], h_banks[c][:].rearrange("m (s r) -> m r s", s=PACK))
@@ -255,7 +253,7 @@ def tile_attend_gpq_sq_x_kernel(tc, xT, cb, norm, ts, y, wt, offs, out):
             seed_targets(c)
         y_weight = keep.tile([P, PACK, P], F32, name="y_weight")
         nc.scalar.activation(y_weight[:], neg_ts[:].rearrange("p (m s) -> p s m", s=PACK), COPY, scale=wt_col(TURNED))
-        for c in range(2, BLOCKS):
+        for c in range(TURNED, BLOCKS):
             make_weights(c, c)
         gather(0)
         turn_k(0, 0)
@@ -273,8 +271,9 @@ def tile_attend_gpq_sq_x_kernel(tc, xT, cb, norm, ts, y, wt, offs, out):
         quantize_k(0, half)
         quantize_x(0)
         quantize_k(half, N)
-        x_bf[2] = keep.tile([P, P, PACK], BF16, name="x_bf2", align_bytes=64)[:]
-        x_bf[3] = keep.tile([P, P, PACK], BF16, name="x_bf3", align_bytes=64)[:]
+        x_second = keep.tile([P, 2, P, PACK], BF16, name="x_second", align_bytes=64)
+        for c in range(2, BLOCKS):
+            x_bf[c] = x_second[:, c - 2]
         interleave_x(3, nc.scalar.copy)
         quantize_x(1)
         interleave_x(2, nc.vector.tensor_copy)
@@ -284,40 +283,43 @@ def tile_attend_gpq_sq_x_kernel(tc, xT, cb, norm, ts, y, wt, offs, out):
         first_product(1, 0, N, 2)
         quantize_x(3)
         quantize_x(2)
-        for c in range(BLOCKS):
+        for c in range(3):
             new_h_bf(c, "h_bf%d" % c)
-        spent_x = late[:, N:].rearrange("p (s c m) -> p c s m", c=2, m=P)
+        spent_x = late[:, N:].rearrange("p (c s m) -> p c s m", c=2, m=P)
         a_terms[0] = spent_x[:, 0]
         weigh(0, 0, half)
         weigh(0, half, N)
-        first_product_by_columns(2, 4)
+        first_product(2, 0, N, 4)
         turn_a(0)
-        y_term_last = keep.tile([P, PACK, P], F32, name="y_term_last", tag="x_bf2", align_bytes=64)
-        nc.gpsimd.tensor_tensor(y_term_last[:], y_last[:].rearrange("p (m s) -> p s m", s=PACK), y_weight[:], MULT)
+
         a_terms[1] = spent_x[:, 1]
         weigh(1, 0, N)
         turn_a(1)
-        first_product_by_columns(3, 2)
-        new_a_term(2, "a_term2")
-        weigh_by_columns(2, 0, P)
+        first_product_by_columns(3, 3)
+        y_term_last = keep.tile([P, PACK, P], F32, name="y_term_last", tag="x_second", align_bytes=64)
+        nc.gpsimd.tensor_tensor(y_term_last[:], y_last[:].rearrange("p (m s) -> p s m", s=PACK), y_weight[:], MULT)
+        new_b_term(2)
+        weigh(2, 0, N)
+        turn_a(2)
         round_h(0)
         round_h(1)
+        round_h(2)
         quantize_kt(2, PACK)
         quantize_h(0)
         second_product(0, 0)
         h_banks.append(bank(1))
         for s in range(PACK):
             nc.tensor.transpose(h_banks[3][:, s * P:(s + 1) * P], y_term_last[:, s], ident[:])
-        add_targets(2, 0, P)
         new_a_term(3, "a_term3")
-        weigh_by_columns(3, 0, P)
+        weigh_by_columns(3)
         quantize_h(1)
-        second_product(1, 3)
+        second_product(1, 2)
         quantize_h(2)
         second_product(2, 4)
-        add_targets(3, 0, P)
+        new_h_bf(3, "h_bf3")
+        add_targets(3)
         quantize_h(3)
-        second_product(3, 2)
+        second_product(3, 3)
         store(0, nc.scalar.copy)
         store(1, nc.scalar.copy)
         store(2, nc.scalar.copy)

@@ -263,6 +263,12 @@ def tile_attend_gpq_sq_x_kernel(tc, xT, cb, norm, ts, y, wt, offs, out):
         gather(2)
         turn_k(2, 2)
         gather(last)
+        warm = bank(4)
+        nc.tensor.transpose(warm[:, 0:P], k_f32[last][:, 1 * P:(1 + 1) * P], ident[:])
+        for i in range(4):
+            nc.tensor.matmul_mx(out=warm[:, P:3 * P], lhsT=kt_codes[:, 0:P].bitcast(E4M3), lhsT_scale=kt_scales[:, 0:P],
+                                rhs=kt_codes[:, 0:half].bitcast(E4M3), rhs_scale=kt_scales[:, 0:half],
+                                start=True, stop=True)
         x_first = keep.tile([P, 2, P, PACK], BF16, name="x_first", align_bytes=64)
         for c in range(2):
             x_bf[c] = x_first[:, c]

@@ -119,11 +119,12 @@ def tile_attend_gpq_sq_x_kernel(tc, xT, cb, norm, ts, y, wt, offs, out):
             for j in range(CHUNKS):
                 n_cols = slice(j * CHUNK, (j + 1) * CHUNK)
                 m_cols = slice(j * CHUNK // PACK, (j + 1) * CHUNK // PACK)
-                src = k_f32[t][:, n_cols].rearrange("p (m s) -> p s m", s=PACK)
+                src = k_f32[t][:, n_cols].rearrange("p (g i s) -> p g s i", i=2, s=PACK)
+                dst = k_cols[:, :, m_cols, t].rearrange("p s (g i) -> p g s i", i=2)
                 if j < CHUNKS // 2:
-                    nc.scalar.copy(k_cols[:, :, m_cols, t], src)
+                    nc.scalar.copy(dst, src)
                 else:
-                    nc.vector.tensor_copy(k_cols[:, :, m_cols, t], src)
+                    nc.vector.tensor_copy(dst, src)
 
         def turn_k(t, w):
             kt_bank = bank(w, BF16)

@@ -18,13 +18,13 @@ COPY = mybir.ActivationFunctionType.Copy
 
 P = 128
 PACK = 4
+RUN = 8
 BLOCKS = R // P
 CHUNK = 128
 CHUNKS = N // CHUNK
 LIST_COLS = CHUNK // 16
 X_HALF = R // 2
-TURNED = 3
-ADD = mybir.AluOpType.add
+EARLY = 2
 
 
 def tile_attend_gpq_sq_x_kernel(tc, xT, cb, norm, ts, y, wt, offs, out):
@@ -32,71 +32,70 @@ def tile_attend_gpq_sq_x_kernel(tc, xT, cb, norm, ts, y, wt, offs, out):
     with ExitStack() as ctx:
         lists = ctx.enter_context(tc.tile_pool(name="lists", bufs=1))
         keep = ctx.enter_context(tc.tile_pool(name="keep", bufs=1))
-        held = ctx.enter_context(tc.psum_pool(name="held", bufs=1))
-        work = ctx.enter_context(tc.psum_pool(name="work", bufs=1))
+        shared = ctx.enter_context(tc.tile_pool(name="shared", bufs=1))
+        psum = ctx.enter_context(tc.psum_pool(name="psum", bufs=1))
 
         def bank(w, dtype=F32):
-            return work.tile([P, N], dtype, name="bank%d" % w)
+            return psum.tile([P, N], dtype, name="bank%d" % w)
+
+        def by_place(natural):
+            return natural.rearrange("p (b s i) -> p s b i", s=PACK, i=RUN)
+
+        def as_dealt(dealt):
+            return dealt.rearrange("p (s b i) -> p s b i", s=PACK, i=RUN)
 
         cb_planes = cb.rearrange("(p t) c -> t p c", t=PACK)
-        windows = {}
-        x_raw = {}
-
-        def load_window(t):
-            windows[t] = keep.tile([P, C], F32, name="window%d" % t)
-            nc.sync.dma_start(windows[t][:], cb_planes[t])
-
-        def load_x(h):
-            if h == 0:
-                x_raw[h] = keep.tile([P, PACK * X_HALF], F32, name="x_raw0", align_bytes=64)[:]
-            else:
-                x_raw[h] = late[:, N // 2:N // 2 + PACK * X_HALF]
-            x_raw[h] = x_raw[h].rearrange("p (t r) -> p t r", t=PACK)
-            nc.sync.dma_start(x_raw[h], x_rows[:, :, h * X_HALF:(h + 1) * X_HALF])
-
-        late = keep.tile([P, 3 * N], F32, name="late", align_bytes=64)
-        offsets = lists.tile([P, N // 16], U16, name="offsets")
-        y_raw = keep.tile([P, TURNED, N], F32, name="y_raw")
-        y_last = keep.tile([P, N], F32, name="y_last")
         x_rows = xT.rearrange("(p t) r -> p t r", t=PACK)
-
+        windows = [keep.tile([P, C], F32, name="window%d" % t) for t in range(PACK)]
+        offsets = lists.tile([P, N // 16], U16, name="offsets")
         rows = keep.tile([P, P], F32, name="rows")
-        nc.gpsimd.memset(rows[:], 0.0)
-        nc.sync.dma_start(y_raw[:], y[0:TURNED * P, :].rearrange("(c p) n -> p c n", p=P))
+        y_early = keep.tile([P, EARLY, N], F32, name="y_early")
+        y_late = [keep.tile([P, N], F32, name="y_late%d" % c) for c in range(EARLY, BLOCKS)]
+        x_low = keep.tile([P, PACK * X_HALF], F32, name="x_low", align_bytes=64)
+        x_high = shared.tile([P, PACK * X_HALF], F32, name="x_high", offset=0, align_bytes=64)
+        x_raw = [half[:].rearrange("p (t r) -> p t r", t=PACK) for half in (x_low, x_high)]
+
+        nc.vector.memset(rows[:], 0.0)
+        nc.sync.dma_start(windows[0][:], cb_planes[0])
         nc.sync.dma_start(rows[0:4, :], norm[0:1, :].rearrange("o (j m) -> (o j) m", m=P))
         nc.sync.dma_start(rows[4:8, :], ts[0:1, :].rearrange("o (j m) -> (o j) m", m=P))
         nc.sync.dma_start(rows[8:12, :], wt.rearrange("(j m) o -> j (m o)", m=P))
-        load_window(0)
         nc.sync.dma_start(offsets[:], offs)
+        nc.sync.dma_start(y_early[:], y[0:EARLY * P, :].rearrange("(c p) n -> p c n", p=P))
         for t in range(1, PACK):
-            load_window(t)
-        load_x(0)
-        load_x(1)
-        nc.sync.dma_start(y_last[:], y[TURNED * P:, :])
+            nc.sync.dma_start(windows[t][:], cb_planes[t])
+        for half in range(2):
+            nc.sync.dma_start(x_raw[half], x_rows[:, :, half * X_HALF:(half + 1) * X_HALF])
+        for c in range(EARLY, BLOCKS):
+            nc.sync.dma_start(y_late[c - EARLY][:], y[c * P:(c + 1) * P, :])
 
         ident = keep.tile([P, P], F32, name="ident")
         make_identity(nc, ident[:])
         ident_bf = keep.tile([P, P], BF16, name="ident_bf")
         nc.vector.tensor_copy(ident_bf[:], ident[:])
-        turned = bank(0)
+        turned = bank(2)
         nc.tensor.transpose(turned[:, 0:P], rows[:], ident[:])
-        cols = keep.tile([P, 16], F32, name="cols")
-        nc.vector.tensor_copy(cols[:], turned[:, 0:16])
+        cols = keep.tile([P, 12], F32, name="cols")
+        nc.vector.tensor_copy(cols[:], turned[:, 0:12])
 
-        norm_bank = bank(1)
-        for j in range(4):
-            nc.tensor.transpose(norm_bank[:, j * P:(j + 1) * P], cols[:, j:j + 1].to_broadcast([P, P]), ident[:])
+        def spread(w, first):
+            spread_bank = bank(w)
+            for j in range(4):
+                nc.tensor.transpose(spread_bank[:, j * P:(j + 1) * P],
+                                    cols[:, first + j:first + j + 1].to_broadcast([P, P]), ident[:])
+            return spread_bank
+
         norm_row = keep.tile([P, N], F32, name="norm_row")
-        nc.scalar.copy(norm_row[:], norm_bank[:])
-        ts_bank = bank(2)
-        for j in range(4):
-            nc.tensor.transpose(ts_bank[:, j * P:(j + 1) * P], cols[:, 4 + j:5 + j].to_broadcast([P, P]), ident[:])
+        nc.scalar.copy(norm_row[:], spread(3, 0)[:])
         neg_ts = keep.tile([P, N], F32, name="neg_ts")
-        nc.scalar.activation(neg_ts[:], ts_bank[:], COPY, scale=-1.0)
+        nc.scalar.activation(as_dealt(neg_ts[:]), by_place(spread(4, 4)[:]), COPY, scale=-1.0)
         ts_sq = keep.tile([P, N], F32, name="ts_sq")
-        nc.vector.tensor_tensor(ts_sq[:].rearrange("p (s m) -> p m s", s=PACK),
-                                neg_ts[:].rearrange("p (m s) -> p m s", s=PACK),
-                                neg_ts[:].rearrange("p (m s) -> p m s", s=PACK), MULT)
+        nc.vector.tensor_tensor(ts_sq[:], neg_ts[:], neg_ts[:], MULT)
+        ts_bank = bank(5)
+        for s in range(PACK):
+            nc.tensor.transpose(ts_bank[:, s * P:(s + 1) * P], neg_ts[:, s * P:(s + 1) * P], ident[:])
+        neg_ts_words = keep.tile([P, P, PACK], F32, name="neg_ts_words")
+        nc.scalar.copy(neg_ts_words[:], ts_bank[:].rearrange("m (s r) -> m r s", s=PACK))
 
         def wt_col(c):
             return cols[:, 8 + c:9 + c]
@@ -106,10 +105,11 @@ def tile_attend_gpq_sq_x_kernel(tc, xT, cb, norm, ts, y, wt, offs, out):
         k_scales = keep.tile([P, N], U8, name="k_scales", align_bytes=64)
         kt_codes = keep.tile([P, D], U32, name="kt_codes", align_bytes=64)
         kt_scales = keep.tile([P, D], U8, name="kt_scales", align_bytes=64)
-        k_cols = k_bf[:].rearrange("p (s m) t -> p s m t", s=PACK)
+        k_dealt = k_bf[:].rearrange("p (s b i) t -> p b s i t", s=PACK, i=RUN)
         k_f32 = [keep.tile([P, N], F32, name="k_f32_%d" % t, align_bytes=64) for t in range(PACK)]
-        kt_early = keep.tile([P, 2 * N], BF16, name="kt_early", align_bytes=64)
-        kt_bf = [kt_early[:], late[:, 0:N].bitcast(BF16)]
+        kt_early = keep.tile([P, 3 * N], BF16, name="kt_early", align_bytes=64)
+        kt_last = shared.tile([P, N], BF16, name="kt_last", offset=0, align_bytes=64)
+        kt_bf = [kt_early[:, t * N:(t + 1) * N] for t in range(PACK - 1)] + [kt_last[:]]
 
         def gather(t):
             for j in range(CHUNKS):
@@ -117,10 +117,8 @@ def tile_attend_gpq_sq_x_kernel(tc, xT, cb, norm, ts, y, wt, offs, out):
                 picked = windows[t][:].indirect(offsets[:, j * LIST_COLS:(j + 1) * LIST_COLS])
                 nc.vector.tensor_tensor(k_f32[t][:, n_cols], picked, norm_row[:, n_cols], MULT)
             for j in range(CHUNKS):
-                n_cols = slice(j * CHUNK, (j + 1) * CHUNK)
-                m_cols = slice(j * CHUNK // PACK, (j + 1) * CHUNK // PACK)
-                src = k_f32[t][:, n_cols].rearrange("p (g i s) -> p g s i", i=2, s=PACK)
-                dst = k_cols[:, :, m_cols, t].rearrange("p s (g i) -> p g s i", i=2)
+                src = k_f32[t][:, j * CHUNK:(j + 1) * CHUNK].rearrange("p (b s i) -> p b s i", s=PACK, i=RUN)
+                dst = k_dealt[:, j * 4:(j + 1) * 4, :, :, t]
                 if j < CHUNKS // 2:
                     nc.scalar.copy(dst, src)
                 else:
@@ -129,108 +127,113 @@ def tile_attend_gpq_sq_x_kernel(tc, xT, cb, norm, ts, y, wt, offs, out):
         def turn_k(t, w):
             kt_bank = bank(w, BF16)
             for s in range(PACK):
-                nc.tensor.transpose(kt_bank[:, s * P:(s + 1) * P], k_cols[:, s, :, t], ident_bf[:])
-            nc.scalar.copy(kt_bf[t // 2][:, (t % 2) * N:(t % 2 + 1) * N].rearrange("m (p s) -> m p s", s=PACK), kt_bank[:].rearrange("m (s p) -> m p s", s=PACK))
+                nc.tensor.transpose(kt_bank[:, s * P:(s + 1) * P], k_bf[:, s * P:(s + 1) * P, t], ident_bf[:])
+            return kt_bank
 
-        def quantize_kt(t_lo, t_hi):
-            d_cols = slice(t_lo * P, t_hi * P)
-            nc.vector.quantize_mx(out=kt_codes[:, d_cols].bitcast(E4M3), scales=kt_scales[:, d_cols],
-                                  in_=kt_bf[t_lo // 2])
+        def copy_kt(t, kt_bank):
+            nc.scalar.copy(kt_bf[t].rearrange("m (p s) -> m p s", s=PACK),
+                           kt_bank[:].rearrange("m (s p) -> m p s", s=PACK))
 
-        h_banks = [held.tile([P, N], F32, name="h_bank%d" % c) for c in range(TURNED)]
+        def quantize_kt(t):
+            d_cols = slice(t * P, (t + 1) * P)
+            nc.vector.quantize_mx(out=kt_codes[:, d_cols].bitcast(E4M3), scales=kt_scales[:, d_cols], in_=kt_bf[t])
 
-        def seed_targets(c):
+        h_banks = {}
+
+        def turn_onto(c, term, first):
+            for s in range(PACK):
+                nc.tensor.matmul(h_banks[c][:, s * P:(s + 1) * P], term[:, s * P:(s + 1) * P], ident[:],
+                                 start=(first and s == 0), stop=(not first and s == PACK - 1), is_transpose=True)
+
+        y_weight = [keep.tile([P, N], F32, name="y_weight%d" % c) for c in range(EARLY + 1)]
+        for c in range(EARLY + 1):
+            nc.scalar.activation(y_weight[c][:], neg_ts[:], COPY, scale=wt_col(c))
+        for c in range(EARLY):
             y_term = keep.tile([P, N], F32, name="y_term%d" % c)
-            nc.vector.scalar_tensor_tensor(
-                y_term[:].rearrange("p (s m) -> p m s", s=PACK),
-                y_raw[:, c, :].rearrange("p (m s) -> p m s", s=PACK),
-                wt_col(c),
-                neg_ts[:].rearrange("p (m s) -> p m s", s=PACK),
-                MULT, MULT)
-            for s in range(PACK):
-                nc.tensor.matmul(h_banks[c][:, s * P:(s + 1) * P], y_term[:, s * P:(s + 1) * P], ident[:],
-                                 start=(s == 0), stop=(c >= TURNED and s == PACK - 1), is_transpose=True)
+            nc.vector.tensor_tensor(as_dealt(y_term[:]), by_place(y_early[:, c, :]), as_dealt(y_weight[c][:]), MULT)
+            h_banks[c] = bank(c)
+            turn_onto(c, y_term, True)
 
-        weights = {}
+        last = PACK - 1
+        for t in range(last):
+            gather(t)
+            copy_kt(t, turn_k(t, 2 + t))
+            quantize_kt(t)
+        gather(last)
 
-        def make_weights(c, w):
-            by_row = keep.tile([P, N], F32, name="by_row%d" % c)
-            nc.scalar.activation(by_row[:], ts_sq[:], COPY, scale=wt_col(c))
-            w_bank = bank(w)
-            for s in range(PACK):
-                nc.tensor.transpose(w_bank[:, s * P:(s + 1) * P], by_row[:, s * P:(s + 1) * P], ident[:])
-            weights[c] = keep.tile([P, N], F32, name="weights%d" % c)
-            nc.scalar.copy(weights[c][:], w_bank[:])
+        warm = bank(2)
+        nc.tensor.transpose(warm[:, 0:P], k_f32[last][:, 0:P], ident[:])
+        for i in range(4):
+            nc.tensor.matmul_mx(out=warm[:, P:3 * P], lhsT=kt_codes[:, 0:P].bitcast(E4M3), lhsT_scale=kt_scales[:, 0:P],
+                                rhs=kt_codes[:, 0:2 * P].bitcast(E4M3), rhs_scale=kt_scales[:, 0:2 * P],
+                                start=True, stop=True)
+        last_kt_bank = turn_k(last, 3)
 
-        x_bf = {}
+        x_pairs = [keep.tile([P, 2, P, PACK], BF16, name="x_pair%d" % half, tag="x_pair%d" % half, align_bytes=64)
+                   for half in range(2)]
         x_codes = [keep.tile([P, P], U32, name="x_codes%d" % c, align_bytes=64) for c in range(BLOCKS)]
         x_scales = [keep.tile([P, P], U8, name="x_scales%d" % c, align_bytes=64) for c in range(BLOCKS)]
-        h_bf = {}
-        h_codes = [keep.tile([P, P], U32, name="h_codes%d" % c, align_bytes=64) for c in range(BLOCKS)]
-        h_scales = [keep.tile([P, P], U8, name="h_scales%d" % c, align_bytes=64) for c in range(BLOCKS)]
-        s_banks = {}
-        o_banks = {}
 
         def interleave_x(c, copy):
             r_cols = slice((c % 2) * P, (c % 2 + 1) * P)
-            copy(x_bf[c].rearrange("p (g i) t -> p g t i", i=4),
+            copy(x_pairs[c // 2][:, c % 2].rearrange("p (g i) t -> p g t i", i=4),
                  x_raw[c // 2][:, :, r_cols].rearrange("p t (g i) -> p g t i", i=4))
 
         def quantize_x(c):
             nc.vector.quantize_mx(out=x_codes[c][:].bitcast(E4M3), scales=x_scales[c][:],
-                                  in_=x_bf[c].rearrange("p r t -> p (r t)"))
+                                  in_=x_pairs[c // 2][:, c % 2].rearrange("p r t -> p (r t)"))
 
-        a_terms = {}
+        interleave_x(0, nc.scalar.copy)
+        interleave_x(1, nc.scalar.copy)
+        interleave_x(3, nc.scalar.copy)
+        nc.vector.quantize_mx(out=k_codes[:].bitcast(E4M3), scales=k_scales[:],
+                              in_=k_bf[:].rearrange("p n t -> p (n t)"))
+        quantize_x(0)
+        quantize_x(1)
+        interleave_x(2, nc.vector.tensor_copy)
+        copy_kt(last, last_kt_bank)
+        quantize_x(3)
+        quantize_x(2)
 
-        def new_a_term(c, tag):
-            a_terms[c] = keep.tile([P, N], F32, name="a_term%d" % c, tag=tag, align_bytes=64)
-
-        def new_b_term(c):
-            a_terms[c] = keep.tile([P, PACK, P], F32, name="a_term%d" % c, align_bytes=64)[:]
-
-        def new_h_bf(c, tag):
-            h_bf[c] = keep.tile([P, P, PACK], BF16, name="h_bf%d" % c, tag=tag, align_bytes=64)
-
-        def quantize_k(lo, hi):
-            nc.vector.quantize_mx(out=k_codes[:, lo:hi].bitcast(E4M3), scales=k_scales[:, lo:hi],
-                                  in_=k_bf[:, lo:hi, :].rearrange("p n t -> p (n t)"))
-
-        def first_product(c, lo, hi, w):
-            s_banks[c, lo] = bank(w)
-            nc.tensor.matmul_mx(out=s_banks[c, lo][:, 0:hi - lo], lhsT=x_codes[c][:].bitcast(E4M3),
-                                lhsT_scale=x_scales[c][:], rhs=k_codes[:, lo:hi].bitcast(E4M3),
-                                rhs_scale=k_scales[:, lo:hi], start=True, stop=True)
-
-        def weigh(c, lo, hi):
-            nc.vector.scalar_tensor_tensor(a_terms[c][:, lo // P:hi // P],
-                                           s_banks[c, lo][:, 0:hi - lo].rearrange("p (s m) -> p s m", m=P), wt_col(c),
-                                           ts_sq[:, lo:hi].rearrange("p (s m) -> p s m", m=P), MULT, MULT)
-
-        def turn_a(c):
-            for s in range(PACK):
-                nc.tensor.matmul(h_banks[c][:, s * P:(s + 1) * P], a_terms[c][:, s], ident[:],
-                                 start=False, stop=(s == PACK - 1), is_transpose=True)
-
-        def first_product_by_columns(c, w):
+        s_banks = {}
+        for c, w in enumerate((2, 4, 5, 6)):
             s_banks[c] = bank(w)
-            for s in range(PACK):
-                n_cols = slice(s * P, (s + 1) * P)
-                nc.tensor.matmul_mx(out=s_banks[c][:, n_cols], lhsT=k_codes[:, n_cols].bitcast(E4M3),
-                                    lhsT_scale=k_scales[:, n_cols], rhs=x_codes[c][:].bitcast(E4M3),
-                                    rhs_scale=x_scales[c][:], start=True, stop=True)
+            nc.tensor.matmul_mx(out=s_banks[c][:], lhsT=x_codes[c][:].bitcast(E4M3), lhsT_scale=x_scales[c][:],
+                                rhs=k_codes[:].bitcast(E4M3), rhs_scale=k_scales[:], start=True, stop=True)
 
-        def weigh_by_columns(c):
-            nc.vector.tensor_tensor(a_terms[c][:], s_banks[c][:], weights[c][:], MULT)
+        y_term2 = keep.tile([P, N], F32, name="y_term2", tag="x_pair1", align_bytes=64)
+        nc.gpsimd.tensor_tensor(as_dealt(y_term2[:]), by_place(y_late[0][:]), as_dealt(y_weight[2][:]), MULT)
+        y_term3 = keep.tile([P, N], F32, name="y_term3")
+        nc.scalar.activation(as_dealt(y_term3[:]), by_place(y_late[1][:]), COPY, scale=wt_col(3))
 
-        def add_targets(c):
-            nc.vector.tensor_tensor(h_bf[c][:].rearrange("m (g i) s -> m g s i", i=4),
-                                    a_terms[c][:].rearrange("m (s g i) -> m g s i", s=PACK, i=4),
-                                    h_banks[c][:].rearrange("m (s g i) -> m g s i", s=PACK, i=4), ADD)
+        a_term2 = keep.tile([P, N], F32, name="a_term2")
+        a_term3 = keep.tile([P, N], F32, name="a_term3", tag="a_term3", align_bytes=64)
+        a_term0 = shared.tile([P, N], F32, name="a_term0", offset=2 * N, align_bytes=64)
+        a_term1 = shared.tile([P, N], F32, name="a_term1", offset=6 * N, align_bytes=64)
+        a_terms = [a_term0[:], a_term1[:], a_term2[:], a_term3[:]]
+        for c in range(BLOCKS):
+            factor = neg_ts if c == BLOCKS - 1 else ts_sq
+            nc.vector.scalar_tensor_tensor(a_terms[c], s_banks[c][:], wt_col(c), factor[:], MULT, MULT)
 
-        def round_h(c):
-            nc.scalar.copy(h_bf[c][:], h_banks[c][:].rearrange("m (s r) -> m r s", s=PACK))
+        turn_onto(0, a_terms[0], False)
+        h_banks[3] = bank(2)
+        turn_onto(3, y_term3, True)
+        turn_onto(1, a_terms[1], False)
+        h_banks[2] = bank(3)
+        turn_onto(2, y_term2, True)
+        turn_onto(2, a_terms[2], False)
+        turn_onto(3, a_terms[3], False)
 
-        def quantize_h(c):
+        h_bf = [keep.tile([P, P, PACK], BF16, name="h_bf%d" % c, align_bytes=64) for c in range(BLOCKS)]
+        h_scales = [keep.tile([P, P], U8, name="h_scales%d" % c, align_bytes=64) for c in range(BLOCKS)]
+        h_codes = {}
+        o_banks = {}
+
+        def h_words(c):
+            return h_banks[c][:].rearrange("m (s r) -> m r s", s=PACK)
+
+        def quantize_h(c, tag):
+            h_codes[c] = keep.tile([P, P], U32, name="h_codes%d" % c, tag=tag, align_bytes=64)
             nc.vector.quantize_mx(out=h_codes[c][:].bitcast(E5M2), scales=h_scales[c][:],
                                   in_=h_bf[c][:].rearrange("m r s -> m (r s)"))
 
@@ -239,95 +242,21 @@ def tile_attend_gpq_sq_x_kernel(tc, xT, cb, norm, ts, y, wt, offs, out):
             nc.tensor.matmul_mx(out=o_banks[c][:], lhsT=h_codes[c][:].bitcast(E5M2), lhsT_scale=h_scales[c][:],
                                 rhs=kt_codes[:].bitcast(E4M3), rhs_scale=kt_scales[:], start=True, stop=True)
 
-        def store(c, copy, pieces=1):
-            width = P // pieces
-            for i in range(pieces):
-                result = keep.tile([P, width, PACK], F32, name="result%d_%d" % (c, i), align_bytes=64,
-                                   tag="result%d_%d" % (c, i))
-                copy(result[:], o_banks[c][:].rearrange("r (t p) -> r p t", t=PACK)[:, i * width:(i + 1) * width, :])
-                nc.sync.dma_start(out[c * P:(c + 1) * P, i * width * PACK:(i + 1) * width * PACK],
-                                  result[:].rearrange("r p t -> r (p t)"))
+        def store(c, copy):
+            result = keep.tile([P, P, PACK], F32, name="result%d" % c, align_bytes=64)
+            copy(result[:], o_banks[c][:].rearrange("r (t p) -> r p t", t=PACK))
+            nc.sync.dma_start(out[c * P:(c + 1) * P, :], result[:].rearrange("r p t -> r (p t)"))
 
-        last = PACK - 1
-        half = N // 2
-        for c in range(TURNED):
-            seed_targets(c)
-        y_weight = keep.tile([P, PACK, P], F32, name="y_weight")
-        nc.scalar.activation(y_weight[:], neg_ts[:].rearrange("p (m s) -> p s m", s=PACK), COPY, scale=wt_col(TURNED))
-        for c in range(TURNED, BLOCKS):
-            make_weights(c, c)
-        gather(0)
-        turn_k(0, 0)
-        gather(1)
-        turn_k(1, 1)
-        quantize_kt(0, 2)
-        gather(2)
-        turn_k(2, 2)
-        gather(last)
-        warm = bank(4)
-        nc.tensor.transpose(warm[:, 0:P], k_f32[last][:, 1 * P:(1 + 1) * P], ident[:])
-        for i in range(4):
-            nc.tensor.matmul_mx(out=warm[:, P:3 * P], lhsT=kt_codes[:, 0:P].bitcast(E4M3), lhsT_scale=kt_scales[:, 0:P],
-                                rhs=kt_codes[:, 0:half].bitcast(E4M3), rhs_scale=kt_scales[:, 0:half],
-                                start=True, stop=True)
-        x_first = keep.tile([P, 2, P, PACK], BF16, name="x_first", align_bytes=64)
-        for c in range(2):
-            x_bf[c] = x_first[:, c]
-        interleave_x(0, nc.scalar.copy)
-        interleave_x(1, nc.scalar.copy)
-        quantize_k(0, half)
-        quantize_x(0)
-        quantize_k(half, N)
-        x_second = keep.tile([P, 2, P, PACK], BF16, name="x_second", align_bytes=64)
-        for c in range(2, BLOCKS):
-            x_bf[c] = x_second[:, c - 2]
-        interleave_x(3, nc.scalar.copy)
-        quantize_x(1)
-        interleave_x(2, nc.vector.tensor_copy)
-        turn_k(last, 3)
-        first_product(0, 0, half, 0)
-        first_product(0, half, N, 1)
-        first_product(1, 0, N, 2)
-        quantize_x(3)
-        quantize_x(2)
-        for c in range(3):
-            new_h_bf(c, "h_bf%d" % c)
-        spent_x = late[:, N:].rearrange("p (c s m) -> p c s m", c=2, m=P)
-        a_terms[0] = spent_x[:, 0]
-        weigh(0, 0, half)
-        weigh(0, half, N)
-        first_product(2, 0, N, 4)
-        turn_a(0)
-
-        a_terms[1] = spent_x[:, 1]
-        weigh(1, 0, N)
-        turn_a(1)
-        first_product_by_columns(3, 3)
-        y_term_last = keep.tile([P, PACK, P], F32, name="y_term_last", tag="x_second", align_bytes=64)
-        nc.gpsimd.tensor_tensor(y_term_last[:], y_last[:].rearrange("p (m s) -> p s m", s=PACK), y_weight[:], MULT)
-        new_b_term(2)
-        weigh(2, 0, N)
-        turn_a(2)
-        round_h(0)
-        round_h(1)
-        round_h(2)
-        quantize_kt(2, PACK)
-        quantize_h(0)
-        second_product(0, 0)
-        h_banks.append(bank(1))
-        for s in range(PACK):
-            nc.tensor.transpose(h_banks[3][:, s * P:(s + 1) * P], y_term_last[:, s], ident[:])
-        new_a_term(3, "a_term3")
-        weigh_by_columns(3)
-        quantize_h(1)
-        second_product(1, 2)
-        quantize_h(2)
-        second_product(2, 4)
-        new_h_bf(3, "h_bf3")
-        add_targets(3)
-        quantize_h(3)
-        second_product(3, 3)
-        store(0, nc.scalar.copy)
-        store(1, nc.scalar.copy)
-        store(2, nc.scalar.copy)
-        store(3, nc.vector.tensor_copy, 2)
+        for c in range(BLOCKS - 1):
+            nc.scalar.copy(h_bf[c][:], h_words(c))
+        quantize_kt(last)
+        quantize_h(0, "h_codes0")
+        quantize_h(1, "h_codes1")
+        nc.vector.tensor_tensor(h_bf[3][:], h_words(3), neg_ts_words[:], MULT)
+        quantize_h(2, "a_term3")
+        quantize_h(3, "h_codes3")
+        for c, w in enumerate((4, 5, 6, 7)):
+            second_product(c, w)
+        for c in range(BLOCKS - 1):
+            store(c, nc.scalar.copy)
+        store(3, nc.vector.tensor_copy)

@@ -18,7 +18,6 @@ COPY = mybir.ActivationFunctionType.Copy
 
 P = 128
 PACK = 4
-RUN = 8
 BLOCKS = R // P
 CHUNK = 128
 CHUNKS = N // CHUNK
@@ -38,11 +37,11 @@ def tile_attend_gpq_sq_x_kernel(tc, xT, cb, norm, ts, y, wt, offs, out):
         def bank(w, dtype=F32):
             return psum.tile([P, N], dtype, name="bank%d" % w)
 
-        def by_place(natural):
-            return natural.rearrange("p (b s i) -> p s b i", s=PACK, i=RUN)
+        def in_words(natural):
+            return natural.rearrange("p (m s) -> p m s", s=PACK)
 
-        def as_dealt(dealt):
-            return dealt.rearrange("p (s b i) -> p s b i", s=PACK, i=RUN)
+        def dealt_in_words(dealt):
+            return dealt.rearrange("p (s m) -> p m s", s=PACK)
 
         cb_planes = cb.rearrange("(p t) c -> t p c", t=PACK)
         x_rows = xT.rearrange("(p t) r -> p t r", t=PACK)
@@ -88,7 +87,7 @@ def tile_attend_gpq_sq_x_kernel(tc, xT, cb, norm, ts, y, wt, offs, out):
         norm_row = keep.tile([P, N], F32, name="norm_row")
         nc.scalar.copy(norm_row[:], spread(3, 0)[:])
         neg_ts = keep.tile([P, N], F32, name="neg_ts")
-        nc.scalar.activation(as_dealt(neg_ts[:]), by_place(spread(4, 4)[:]), COPY, scale=-1.0)
+        nc.scalar.activation(dealt_in_words(neg_ts[:]), in_words(spread(4, 4)[:]), COPY, scale=-1.0)
         ts_sq = keep.tile([P, N], F32, name="ts_sq")
         nc.vector.tensor_tensor(ts_sq[:], neg_ts[:], neg_ts[:], MULT)
         ts_bank = bank(5)
@@ -105,7 +104,7 @@ def tile_attend_gpq_sq_x_kernel(tc, xT, cb, norm, ts, y, wt, offs, out):
         k_scales = keep.tile([P, N], U8, name="k_scales", align_bytes=64)
         kt_codes = keep.tile([P, D], U32, name="kt_codes", align_bytes=64)
         kt_scales = keep.tile([P, D], U8, name="kt_scales", align_bytes=64)
-        k_dealt = k_bf[:].rearrange("p (s b i) t -> p b s i t", s=PACK, i=RUN)
+        k_dealt = k_bf[:].rearrange("p (s g i) t -> p g s i t", s=PACK, i=2)
         k_f32 = [keep.tile([P, N], F32, name="k_f32_%d" % t, align_bytes=64) for t in range(PACK)]
         kt_early = keep.tile([P, 3 * N], BF16, name="kt_early", align_bytes=64)
         kt_last = shared.tile([P, N], BF16, name="kt_last", offset=0, align_bytes=64)
@@ -117,8 +116,8 @@ def tile_attend_gpq_sq_x_kernel(tc, xT, cb, norm, ts, y, wt, offs, out):
                 picked = windows[t][:].indirect(offsets[:, j * LIST_COLS:(j + 1) * LIST_COLS])
                 nc.vector.tensor_tensor(k_f32[t][:, n_cols], picked, norm_row[:, n_cols], MULT)
             for j in range(CHUNKS):
-                src = k_f32[t][:, j * CHUNK:(j + 1) * CHUNK].rearrange("p (b s i) -> p b s i", s=PACK, i=RUN)
-                dst = k_dealt[:, j * 4:(j + 1) * 4, :, :, t]
+                src = k_f32[t][:, j * CHUNK:(j + 1) * CHUNK].rearrange("p (g i s) -> p g s i", i=2, s=PACK)
+                dst = k_dealt[:, j * 16:(j + 1) * 16, :, :, t]
                 if j < CHUNKS // 2:
                     nc.scalar.copy(dst, src)
                 else:
@@ -150,7 +149,8 @@ def tile_attend_gpq_sq_x_kernel(tc, xT, cb, norm, ts, y, wt, offs, out):
             nc.scalar.activation(y_weight[c][:], neg_ts[:], COPY, scale=wt_col(c))
         for c in range(EARLY):
             y_term = keep.tile([P, N], F32, name="y_term%d" % c)
-            nc.vector.tensor_tensor(as_dealt(y_term[:]), by_place(y_early[:, c, :]), as_dealt(y_weight[c][:]), MULT)
+            nc.vector.tensor_tensor(dealt_in_words(y_term[:]), in_words(y_early[:, c, :]),
+                                    dealt_in_words(y_weight[c][:]), MULT)
             h_banks[c] = bank(c)
             turn_onto(c, y_term, True)
 
@@ -202,9 +202,11 @@ def tile_attend_gpq_sq_x_kernel(tc, xT, cb, norm, ts, y, wt, offs, out):
                                 rhs=k_codes[:].bitcast(E4M3), rhs_scale=k_scales[:], start=True, stop=True)
 
         y_term2 = keep.tile([P, N], F32, name="y_term2", tag="x_pair1", align_bytes=64)
-        nc.gpsimd.tensor_tensor(as_dealt(y_term2[:]), by_place(y_late[0][:]), as_dealt(y_weight[2][:]), MULT)
+        nc.gpsimd.tensor_tensor(y_term2[:].rearrange("p (s m) -> p s m", s=PACK),
+                                y_late[0][:].rearrange("p (m s) -> p s m", s=PACK),
+                                y_weight[2][:].rearrange("p (s m) -> p s m", s=PACK), MULT)
         y_term3 = keep.tile([P, N], F32, name="y_term3")
-        nc.scalar.activation(as_dealt(y_term3[:]), by_place(y_late[1][:]), COPY, scale=wt_col(3))
+        nc.scalar.activation(dealt_in_words(y_term3[:]), in_words(y_late[1][:]), COPY, scale=wt_col(3))
 
         a_term2 = keep.tile([P, N], F32, name="a_term2")
         a_term3 = keep.tile([P, N], F32, name="a_term3", tag="a_term3", align_bytes=64)

@@ -55,12 +55,12 @@ def tile_attend_gpq_sq_x_kernel(tc, xT, cb, norm, ts, y, wt, offs, out):
         x_raw = [half[:].rearrange("p (t r) -> p t r", t=PACK) for half in (x_low, x_high)]
 
         nc.vector.memset(rows[:], 0.0)
-        nc.sync.dma_start(windows[0][:], cb_planes[0])
+        nc.sync.dma_start(y_early[:], y[0:EARLY * P, :].rearrange("(c p) n -> p c n", p=P))
         nc.sync.dma_start(rows[0:4, :], norm[0:1, :].rearrange("o (j m) -> (o j) m", m=P))
         nc.sync.dma_start(rows[4:8, :], ts[0:1, :].rearrange("o (j m) -> (o j) m", m=P))
         nc.sync.dma_start(rows[8:12, :], wt.rearrange("(j m) o -> j (m o)", m=P))
+        nc.sync.dma_start(windows[0][:], cb_planes[0])
         nc.sync.dma_start(offsets[:], offs)
-        nc.sync.dma_start(y_early[:], y[0:EARLY * P, :].rearrange("(c p) n -> p c n", p=P))
         for t in range(1, PACK):
             nc.sync.dma_start(windows[t][:], cb_planes[t])
         for half in range(2):
@@ -144,13 +144,16 @@ def tile_attend_gpq_sq_x_kernel(tc, xT, cb, norm, ts, y, wt, offs, out):
                 nc.tensor.matmul(h_banks[c][:, s * P:(s + 1) * P], term[:, s * P:(s + 1) * P], ident[:],
                                  start=(first and s == 0), stop=(not first and s == PACK - 1), is_transpose=True)
 
-        y_weight = [keep.tile([P, N], F32, name="y_weight%d" % c) for c in range(EARLY + 1)]
-        for c in range(EARLY + 1):
-            nc.scalar.activation(y_weight[c][:], neg_ts[:], COPY, scale=wt_col(c))
+        y_weight = keep.tile([P, N], F32, name="y_weight")
+        nc.scalar.activation(y_weight[:], neg_ts[:], COPY, scale=wt_col(2))
+        s_weight = [keep.tile([P, N], F32, name="s_weight%d" % c) for c in range(BLOCKS)]
+        for c in range(BLOCKS):
+            factor = neg_ts if c == BLOCKS - 1 else ts_sq
+            nc.vector.tensor_scalar_mul(s_weight[c][:], factor[:], wt_col(c))
         for c in range(EARLY):
             y_term = keep.tile([P, N], F32, name="y_term%d" % c)
-            nc.vector.tensor_tensor(dealt_in_words(y_term[:]), in_words(y_early[:, c, :]),
-                                    dealt_in_words(y_weight[c][:]), MULT)
+            nc.vector.scalar_tensor_tensor(dealt_in_words(y_term[:]), in_words(y_early[:, c, :]), wt_col(c),
+                                           dealt_in_words(neg_ts[:]), MULT, MULT)
             h_banks[c] = bank(c)
             turn_onto(c, y_term, True)
 
@@ -204,7 +207,7 @@ def tile_attend_gpq_sq_x_kernel(tc, xT, cb, norm, ts, y, wt, offs, out):
         y_term2 = keep.tile([P, N], F32, name="y_term2", tag="x_pair1", align_bytes=64)
         nc.gpsimd.tensor_tensor(y_term2[:].rearrange("p (s m) -> p s m", s=PACK),
                                 y_late[0][:].rearrange("p (m s) -> p s m", s=PACK),
-                                y_weight[2][:].rearrange("p (s m) -> p s m", s=PACK), MULT)
+                                y_weight[:].rearrange("p (s m) -> p s m", s=PACK), MULT)
         y_term3 = keep.tile([P, N], F32, name="y_term3")
         nc.scalar.activation(dealt_in_words(y_term3[:]), in_words(y_late[1][:]), COPY, scale=wt_col(3))
 
@@ -214,16 +217,15 @@ def tile_attend_gpq_sq_x_kernel(tc, xT, cb, norm, ts, y, wt, offs, out):
         a_term1 = shared.tile([P, N], F32, name="a_term1", offset=6 * N, align_bytes=64)
         a_terms = [a_term0[:], a_term1[:], a_term2[:], a_term3[:]]
         for c in range(BLOCKS):
-            factor = neg_ts if c == BLOCKS - 1 else ts_sq
-            nc.vector.scalar_tensor_tensor(a_terms[c], s_banks[c][:], wt_col(c), factor[:], MULT, MULT)
+            nc.vector.tensor_tensor(a_terms[c], s_banks[c][:], s_weight[c][:], MULT)
 
         turn_onto(0, a_terms[0], False)
         h_banks[3] = bank(2)
         turn_onto(3, y_term3, True)
         turn_onto(1, a_terms[1], False)
         h_banks[2] = bank(3)
-        turn_onto(2, y_term2, True)
-        turn_onto(2, a_terms[2], False)
+        turn_onto(2, a_terms[2], True)
+        turn_onto(2, y_term2, False)
         turn_onto(3, a_terms[3], False)
 
         h_bf = [keep.tile([P, P, PACK], BF16, name="h_bf%d" % c, align_bytes=64) for c in range(BLOCKS)]

@@ -165,7 +165,7 @@ def tile_attend_gpq_sq_x_kernel(tc, xT, cb, norm, ts, y, wt, offs, out):
         gather(last)
 
         warm = bank(2)
-        nc.tensor.transpose(warm[:, 0:P], k_f32[last][:, 0:P], ident[:])
+        nc.tensor.transpose(warm[:, 0:P], k_f32[last][:, P:2 * P], ident[:])
         for i in range(4):
             nc.tensor.matmul_mx(out=warm[:, P:3 * P], lhsT=kt_codes[:, 0:P].bitcast(E4M3), lhsT_scale=kt_scales[:, 0:P],
                                 rhs=kt_codes[:, 0:2 * P].bitcast(E4M3), rhs_scale=kt_scales[:, 0:2 * P],
@@ -189,8 +189,11 @@ def tile_attend_gpq_sq_x_kernel(tc, xT, cb, norm, ts, y, wt, offs, out):
         interleave_x(0, nc.scalar.copy)
         interleave_x(1, nc.scalar.copy)
         interleave_x(3, nc.scalar.copy)
-        nc.vector.quantize_mx(out=k_codes[:].bitcast(E4M3), scales=k_scales[:],
-                              in_=k_bf[:].rearrange("p n t -> p (n t)"))
+        for half in range(2):
+            for s in range(PACK):
+                n_cols = slice(s * P + half * P // 2, s * P + (half + 1) * P // 2)
+                nc.vector.quantize_mx(out=k_codes[:, n_cols].bitcast(E4M3), scales=k_scales[:, n_cols],
+                                      in_=k_bf[:, n_cols, :].rearrange("p n t -> p (n t)"))
         quantize_x(0)
         quantize_x(1)
         interleave_x(2, nc.vector.tensor_copy)

@@ -14,6 +14,7 @@ U8 = mybir.dt.uint8
 E4M3 = mybir.dt.float8_e4m3fn_x4
 E5M2 = mybir.dt.float8_e5m2_x4
 MULT = mybir.AluOpType.mult
+ADD = mybir.AluOpType.add
 COPY = mybir.ActivationFunctionType.Copy
 
 P = 128
@@ -145,11 +146,16 @@ def tile_attend_gpq_sq_x_kernel(tc, xT, cb, norm, ts, y, wt, offs, out):
                                  start=(first and s == 0), stop=(not first and s == PACK - 1), is_transpose=True)
 
         y_weight = keep.tile([P, N], F32, name="y_weight")
-        nc.scalar.activation(y_weight[:], neg_ts[:], COPY, scale=wt_col(2))
+        nc.scalar.activation(y_weight[:], neg_ts[:], COPY, scale=wt_col(3))
         s_weight = [keep.tile([P, N], F32, name="s_weight%d" % c) for c in range(BLOCKS)]
         for c in range(BLOCKS):
-            factor = neg_ts if c == BLOCKS - 1 else ts_sq
+            factor = neg_ts if c == 2 else ts_sq
             nc.vector.tensor_scalar_mul(s_weight[c][:], factor[:], wt_col(c))
+        weight_bank = bank(6)
+        for s in range(PACK):
+            nc.tensor.transpose(weight_bank[:, s * P:(s + 1) * P], s_weight[3][:, s * P:(s + 1) * P], ident[:])
+        turned_weight = keep.tile([P, N], F32, name="turned_weight")
+        nc.scalar.copy(turned_weight[:], weight_bank[:])
         for c in range(EARLY):
             y_term = keep.tile([P, N], F32, name="y_term%d" % c)
             nc.vector.scalar_tensor_tensor(dealt_in_words(y_term[:]), in_words(y_early[:, c, :]), wt_col(c),
@@ -197,39 +203,46 @@ def tile_attend_gpq_sq_x_kernel(tc, xT, cb, norm, ts, y, wt, offs, out):
         quantize_x(0)
         quantize_x(1)
         interleave_x(2, nc.vector.tensor_copy)
+        y_term2 = keep.tile([P, N], F32, name="y_term2")
+        nc.scalar.activation(dealt_in_words(y_term2[:]), in_words(y_late[0][:]), COPY, scale=wt_col(2))
         copy_kt(last, last_kt_bank)
         quantize_x(3)
         quantize_x(2)
 
         s_banks = {}
-        for c, w in enumerate((2, 4, 5, 6)):
+        for c, w in enumerate((2, 4, 5)):
             s_banks[c] = bank(w)
             nc.tensor.matmul_mx(out=s_banks[c][:], lhsT=x_codes[c][:].bitcast(E4M3), lhsT_scale=x_scales[c][:],
                                 rhs=k_codes[:].bitcast(E4M3), rhs_scale=k_scales[:], start=True, stop=True)
+        s_banks[3] = bank(6)
+        for s in range(PACK):
+            n_cols = slice(s * P, (s + 1) * P)
+            nc.tensor.matmul_mx(out=s_banks[3][:, n_cols], lhsT=k_codes[:, n_cols].bitcast(E4M3),
+                                lhsT_scale=k_scales[:, n_cols], rhs=x_codes[3][:].bitcast(E4M3),
+                                rhs_scale=x_scales[3][:], start=True, stop=True)
 
-        y_term2 = keep.tile([P, N], F32, name="y_term2", tag="x_pair1", align_bytes=64)
-        nc.gpsimd.tensor_tensor(y_term2[:].rearrange("p (s m) -> p s m", s=PACK),
-                                y_late[0][:].rearrange("p (m s) -> p s m", s=PACK),
+        y_term3 = keep.tile([P, N], F32, name="y_term3", tag="x_pair1", align_bytes=64)
+        nc.gpsimd.tensor_tensor(y_term3[:].rearrange("p (s m) -> p s m", s=PACK),
+                                y_late[1][:].rearrange("p (m s) -> p s m", s=PACK),
                                 y_weight[:].rearrange("p (s m) -> p s m", s=PACK), MULT)
-        y_term3 = keep.tile([P, N], F32, name="y_term3")
-        nc.scalar.activation(dealt_in_words(y_term3[:]), in_words(y_late[1][:]), COPY, scale=wt_col(3))
 
         a_term2 = keep.tile([P, N], F32, name="a_term2")
-        a_term3 = keep.tile([P, N], F32, name="a_term3", tag="a_term3", align_bytes=64)
+        a_term3 = keep.tile([P, N], F32, name="a_term3")
         a_term0 = shared.tile([P, N], F32, name="a_term0", offset=2 * N, align_bytes=64)
         a_term1 = shared.tile([P, N], F32, name="a_term1", offset=6 * N, align_bytes=64)
         a_terms = [a_term0[:], a_term1[:], a_term2[:], a_term3[:]]
         for c in range(BLOCKS):
-            nc.vector.tensor_tensor(a_terms[c], s_banks[c][:], s_weight[c][:], MULT)
+            weight = s_weight[c] if c < 3 else turned_weight
+            nc.vector.tensor_tensor(a_terms[c], s_banks[c][:], weight[:], MULT)
 
-        turn_onto(0, a_terms[0], False)
-        h_banks[3] = bank(2)
-        turn_onto(3, y_term3, True)
-        turn_onto(1, a_terms[1], False)
-        h_banks[2] = bank(3)
-        turn_onto(2, a_terms[2], True)
-        turn_onto(2, y_term2, False)
-        turn_onto(3, a_terms[3], False)
+        for c in range(EARLY):
+            turn_onto(c, a_terms[c], False)
+        h_banks[3] = bank(3)
+        for s in range(PACK):
+            nc.tensor.transpose(h_banks[3][:, s * P:(s + 1) * P], y_term3[:, s * P:(s + 1) * P], ident[:])
+        h_banks[2] = bank(5)
+        turn_onto(2, y_term2, True)
+        turn_onto(2, a_terms[2], False)
 
         h_bf = [keep.tile([P, P, PACK], BF16, name="h_bf%d" % c, align_bytes=64) for c in range(BLOCKS)]
         h_scales = [keep.tile([P, P], U8, name="h_scales%d" % c, align_bytes=64) for c in range(BLOCKS)]
@@ -254,16 +267,19 @@ def tile_attend_gpq_sq_x_kernel(tc, xT, cb, norm, ts, y, wt, offs, out):
             copy(result[:], o_banks[c][:].rearrange("r (t p) -> r p t", t=PACK))
             nc.sync.dma_start(out[c * P:(c + 1) * P, :], result[:].rearrange("r p t -> r (p t)"))
 
-        for c in range(BLOCKS - 1):
+        for c in range(EARLY):
             nc.scalar.copy(h_bf[c][:], h_words(c))
         quantize_kt(last)
         quantize_h(0, "h_codes0")
+        nc.vector.tensor_tensor(h_bf[3][:].rearrange("m (g i) s -> m g s i", i=4),
+                                a_terms[3].rearrange("m (s g i) -> m g s i", s=PACK, i=4),
+                                h_banks[3][:].rearrange("m (s g i) -> m g s i", s=PACK, i=4), ADD)
         quantize_h(1, "h_codes1")
-        nc.vector.tensor_tensor(h_bf[3][:], h_words(3), neg_ts_words[:], MULT)
-        quantize_h(2, "a_term3")
+        nc.vector.tensor_tensor(h_bf[2][:], h_words(2), neg_ts_words[:], MULT)
         quantize_h(3, "h_codes3")
-        for c, w in enumerate((4, 5, 6, 7)):
+        quantize_h(2, "h_codes2")
+        for c, w in ((0, 2), (1, 4), (3, 6), (2, 7)):
             second_product(c, w)
-        for c in range(BLOCKS - 1):
+        for c in (0, 1, 3):
             store(c, nc.scalar.copy)
-        store(3, nc.vector.tensor_copy)
+        store(2, nc.vector.tensor_copy)

@@ -24,6 +24,7 @@ CHUNK = 128
 CHUNKS = N // CHUNK
 LIST_COLS = CHUNK // 16
 X_HALF = R // 2
+D_HALF = D // 2
 EARLY = 2
 
 
@@ -135,8 +136,10 @@ def tile_attend_gpq_sq_x_kernel(tc, xT, cb, norm, ts, y, wt, offs, out):
                            kt_bank[:].rearrange("m (s p) -> m p s", s=PACK))
 
         def quantize_kt(t):
-            d_cols = slice(t * P, (t + 1) * P)
-            nc.vector.quantize_mx(out=kt_codes[:, d_cols].bitcast(E4M3), scales=kt_scales[:, d_cols], in_=kt_bf[t])
+            for half in range(2):
+                d_cols = slice(half * D_HALF + t * P // 2, half * D_HALF + (t + 1) * P // 2)
+                nc.vector.quantize_mx(out=kt_codes[:, d_cols].bitcast(E4M3), scales=kt_scales[:, d_cols],
+                                      in_=kt_bf[t][:, half * N // 2:(half + 1) * N // 2])
 
         h_banks = {}
 
@@ -172,9 +175,9 @@ def tile_attend_gpq_sq_x_kernel(tc, xT, cb, norm, ts, y, wt, offs, out):
 
         warm = bank(2)
         nc.tensor.transpose(warm[:, 0:P], k_f32[last][:, P:2 * P], ident[:])
-        for i in range(4):
-            nc.tensor.matmul_mx(out=warm[:, P:3 * P], lhsT=kt_codes[:, 0:P].bitcast(E4M3), lhsT_scale=kt_scales[:, 0:P],
-                                rhs=kt_codes[:, 0:2 * P].bitcast(E4M3), rhs_scale=kt_scales[:, 0:2 * P],
+        for i in range(8):
+            nc.tensor.matmul_mx(out=warm[:, P:2 * P], lhsT=kt_codes[:, 0:P].bitcast(E4M3), lhsT_scale=kt_scales[:, 0:P],
+                                rhs=kt_codes[:, 0:P].bitcast(E4M3), rhs_scale=kt_scales[:, 0:P],
                                 start=True, stop=True)
         last_kt_bank = turn_k(last, 3)
 
@@ -257,14 +260,19 @@ def tile_attend_gpq_sq_x_kernel(tc, xT, cb, norm, ts, y, wt, offs, out):
             nc.vector.quantize_mx(out=h_codes[c][:].bitcast(E5M2), scales=h_scales[c][:],
                                   in_=h_bf[c][:].rearrange("m r s -> m (r s)"))
 
-        def second_product(c, w):
-            o_banks[c] = bank(w)
-            nc.tensor.matmul_mx(out=o_banks[c][:], lhsT=h_codes[c][:].bitcast(E5M2), lhsT_scale=h_scales[c][:],
-                                rhs=kt_codes[:].bitcast(E4M3), rhs_scale=kt_scales[:], start=True, stop=True)
+        def second_product(c, banks):
+            for half, w in enumerate(banks):
+                d_cols = slice(half * D_HALF, (half + 1) * D_HALF)
+                o_banks[c, half] = bank(w)
+                nc.tensor.matmul_mx(out=o_banks[c, half][:, 0:D_HALF], lhsT=h_codes[c][:].bitcast(E5M2),
+                                    lhsT_scale=h_scales[c][:], rhs=kt_codes[:, d_cols].bitcast(E4M3),
+                                    rhs_scale=kt_scales[:, d_cols], start=True, stop=True)
 
-        def store(c, copy):
+        def store(c, copies):
             result = keep.tile([P, P, PACK], F32, name="result%d" % c, align_bytes=64)
-            copy(result[:], o_banks[c][:].rearrange("r (t p) -> r p t", t=PACK))
+            for half, copy in enumerate(copies):
+                copy(result[:, half * P // 2:(half + 1) * P // 2, :],
+                     o_banks[c, half][:, 0:D_HALF].rearrange("r (t p) -> r p t", t=PACK))
             nc.sync.dma_start(out[c * P:(c + 1) * P, :], result[:].rearrange("r p t -> r (p t)"))
 
         for c in range(EARLY):
@@ -278,8 +286,8 @@ def tile_attend_gpq_sq_x_kernel(tc, xT, cb, norm, ts, y, wt, offs, out):
         nc.vector.tensor_tensor(h_bf[2][:], h_words(2), neg_ts_words[:], MULT)
         quantize_h(3, "h_codes3")
         quantize_h(2, "h_codes2")
-        for c, w in ((0, 2), (1, 4), (3, 6), (2, 7)):
-            second_product(c, w)
-        for c in (0, 1, 3):
-            store(c, nc.scalar.copy)
-        store(2, nc.vector.tensor_copy)
+        for c, banks in ((0, (2, 4)), (1, (6, 7)), (3, (0, 1)), (2, (3, 5))):
+            second_product(c, banks)
+        store(0, (nc.scalar.copy, nc.scalar.copy))
+        for c in (1, 3, 2):
+            store(c, (nc.scalar.copy, nc.vector.tensor_copy))

@@ -53,7 +53,7 @@ def tile_attend_gpq_sq_x_kernel(tc, xT, cb, norm, ts, y, wt, offs, out):
         y_early = keep.tile([P, EARLY, N], F32, name="y_early")
         y_late = [keep.tile([P, N], F32, name="y_late%d" % c) for c in range(EARLY, BLOCKS)]
         x_low = keep.tile([P, PACK * X_HALF], F32, name="x_low", align_bytes=64)
-        x_high = shared.tile([P, PACK * X_HALF], F32, name="x_high", offset=0, align_bytes=64)
+        x_high = shared.tile([P, PACK * X_HALF], F32, name="x_high", offset=2 * N, align_bytes=64)
         x_raw = [half[:].rearrange("p (t r) -> p t r", t=PACK) for half in (x_low, x_high)]
 
         nc.vector.memset(rows[:], 0.0)
@@ -108,9 +108,9 @@ def tile_attend_gpq_sq_x_kernel(tc, xT, cb, norm, ts, y, wt, offs, out):
         kt_scales = keep.tile([P, D], U8, name="kt_scales", align_bytes=64)
         k_dealt = k_bf[:].rearrange("p (s g i) t -> p g s i t", s=PACK, i=2)
         k_f32 = [keep.tile([P, N], F32, name="k_f32_%d" % t, align_bytes=64) for t in range(PACK)]
-        kt_early = keep.tile([P, 3 * N], BF16, name="kt_early", align_bytes=64)
-        kt_last = shared.tile([P, N], BF16, name="kt_last", offset=0, align_bytes=64)
-        kt_bf = [kt_early[:, t * N:(t + 1) * N] for t in range(PACK - 1)] + [kt_last[:]]
+        kt_early = keep.tile([P, 2, 2, P // 2, PACK], BF16, name="kt_early", align_bytes=64)
+        kt_late = shared.tile([P, 2, 2, P // 2, PACK], BF16, name="kt_late", offset=0, align_bytes=64)
+        kt_pairs = [kt_early, kt_late]
 
         def gather(t):
             for j in range(CHUNKS):
@@ -132,14 +132,14 @@ def tile_attend_gpq_sq_x_kernel(tc, xT, cb, norm, ts, y, wt, offs, out):
             return kt_bank
 
         def copy_kt(t, kt_bank):
-            nc.scalar.copy(kt_bf[t].rearrange("m (p s) -> m p s", s=PACK),
-                           kt_bank[:].rearrange("m (s p) -> m p s", s=PACK))
+            nc.scalar.copy(kt_pairs[t // 2][:, :, t % 2], kt_bank[:].rearrange("m (s h p) -> m h p s", s=PACK, h=2))
 
-        def quantize_kt(t):
+        def quantize_kt(pair):
             for half in range(2):
-                d_cols = slice(half * D_HALF + t * P // 2, half * D_HALF + (t + 1) * P // 2)
+                place = 2 + pair if half else 1 - pair
+                d_cols = slice(place * P, (place + 1) * P)
                 nc.vector.quantize_mx(out=kt_codes[:, d_cols].bitcast(E4M3), scales=kt_scales[:, d_cols],
-                                      in_=kt_bf[t][:, half * N // 2:(half + 1) * N // 2])
+                                      in_=kt_pairs[pair][:, half].rearrange("m t p s -> m (t p s)"))
 
         h_banks = {}
 
@@ -167,17 +167,20 @@ def tile_attend_gpq_sq_x_kernel(tc, xT, cb, norm, ts, y, wt, offs, out):
             turn_onto(c, y_term, True)
 
         last = PACK - 1
-        for t in range(last):
+        for t in range(2):
             gather(t)
             copy_kt(t, turn_k(t, 2 + t))
-            quantize_kt(t)
+        quantize_kt(0)
+        gather(2)
+        held_kt_bank = turn_k(2, 7)
         gather(last)
 
         warm = bank(2)
         nc.tensor.transpose(warm[:, 0:P], k_f32[last][:, P:2 * P], ident[:])
-        for i in range(8):
-            nc.tensor.matmul_mx(out=warm[:, P:2 * P], lhsT=kt_codes[:, 0:P].bitcast(E4M3), lhsT_scale=kt_scales[:, 0:P],
-                                rhs=kt_codes[:, 0:P].bitcast(E4M3), rhs_scale=kt_scales[:, 0:P],
+        for i in range(4):
+            nc.tensor.matmul_mx(out=warm[:, P:3 * P], lhsT=kt_codes[:, P:2 * P].bitcast(E4M3),
+                                lhsT_scale=kt_scales[:, P:2 * P], rhs=kt_codes[:, P:3 * P].bitcast(E4M3),
+                                rhs_scale=kt_scales[:, P:3 * P],
                                 start=True, stop=True)
         last_kt_bank = turn_k(last, 3)
 
@@ -209,6 +212,7 @@ def tile_attend_gpq_sq_x_kernel(tc, xT, cb, norm, ts, y, wt, offs, out):
         y_term2 = keep.tile([P, N], F32, name="y_term2")
         nc.scalar.activation(dealt_in_words(y_term2[:]), in_words(y_late[0][:]), COPY, scale=wt_col(2))
         copy_kt(last, last_kt_bank)
+        copy_kt(2, held_kt_bank)
         quantize_x(3)
         quantize_x(2)
 
@@ -231,8 +235,8 @@ def tile_attend_gpq_sq_x_kernel(tc, xT, cb, norm, ts, y, wt, offs, out):
 
         a_term2 = keep.tile([P, N], F32, name="a_term2")
         a_term3 = keep.tile([P, N], F32, name="a_term3")
-        a_term0 = shared.tile([P, N], F32, name="a_term0", offset=2 * N, align_bytes=64)
-        a_term1 = shared.tile([P, N], F32, name="a_term1", offset=6 * N, align_bytes=64)
+        a_term0 = shared.tile([P, N], F32, name="a_term0", offset=4 * N, align_bytes=64)
+        a_term1 = shared.tile([P, N], F32, name="a_term1", offset=8 * N, align_bytes=64)
         a_terms = [a_term0[:], a_term1[:], a_term2[:], a_term3[:]]
         for c in range(BLOCKS):
             weight = s_weight[c] if c < 3 else turned_weight
@@ -271,13 +275,14 @@ def tile_attend_gpq_sq_x_kernel(tc, xT, cb, norm, ts, y, wt, offs, out):
         def store(c, copies):
             result = keep.tile([P, P, PACK], F32, name="result%d" % c, align_bytes=64)
             for half, copy in enumerate(copies):
-                copy(result[:, half * P // 2:(half + 1) * P // 2, :],
-                     o_banks[c, half][:, 0:D_HALF].rearrange("r (t p) -> r p t", t=PACK))
+                by_pair = o_banks[c, half][:, 0:D_HALF].rearrange("r (u e p) -> r p u e", u=2, e=2)
+                copy(result[:, half * P // 2:(half + 1) * P // 2, :].rearrange("r p (u e) -> r p u e", e=2),
+                     by_pair if half else by_pair[:, :, ::-1, :])
             nc.sync.dma_start(out[c * P:(c + 1) * P, :], result[:].rearrange("r p t -> r (p t)"))
 
         for c in range(EARLY):
             nc.scalar.copy(h_bf[c][:], h_words(c))
-        quantize_kt(last)
+        quantize_kt(1)
         quantize_h(0, "h_codes0")
         nc.vector.tensor_tensor(h_bf[3][:].rearrange("m (g i) s -> m g s i", i=4),
                                 a_terms[3].rearrange("m (s g i) -> m g s i", s=PACK, i=4),

from contextlib import ExitStack

import concourse.mybir as mybir
from concourse.masks import make_identity

N, C, D, R = 512, 4096, 512, 512
FLOPS = 2 * 2 * R * N * D

F32 = mybir.dt.float32
BF16 = mybir.dt.bfloat16
U32 = mybir.dt.uint32
U16 = mybir.dt.uint16
U8 = mybir.dt.uint8
E4M3 = mybir.dt.float8_e4m3fn_x4
E5M2 = mybir.dt.float8_e5m2_x4
MULT = mybir.AluOpType.mult
ADD = mybir.AluOpType.add
COPY = mybir.ActivationFunctionType.Copy

P = 128
PACK = 4
BLOCKS = R // P
CHUNK = 128
CHUNKS = N // CHUNK
LIST_COLS = CHUNK // 16
X_HALF = R // 2
D_HALF = D // 2
EARLY = 2


def tile_attend_gpq_sq_x_kernel(tc, xT, cb, norm, ts, y, wt, offs, out):
    nc = tc.nc
    with ExitStack() as ctx:
        lists = ctx.enter_context(tc.tile_pool(name="lists", bufs=1))
        keep = ctx.enter_context(tc.tile_pool(name="keep", bufs=1))
        shared = ctx.enter_context(tc.tile_pool(name="shared", bufs=1))
        psum = ctx.enter_context(tc.psum_pool(name="psum", bufs=1))

        def bank(w, dtype=F32):
            return psum.tile([P, N], dtype, name="bank%d" % w)

        def in_words(natural):
            return natural.rearrange("p (m s) -> p m s", s=PACK)

        def dealt_in_words(dealt):
            return dealt.rearrange("p (s m) -> p m s", s=PACK)

        cb_planes = cb.rearrange("(p t) c -> t p c", t=PACK)
        x_rows = xT.rearrange("(p t) r -> p t r", t=PACK)
        windows = [keep.tile([P, C], F32, name="window%d" % t) for t in range(PACK)]
        offsets = lists.tile([P, N // 16], U16, name="offsets")
        rows = keep.tile([P, P], F32, name="rows")
        y_early = keep.tile([P, EARLY, N], F32, name="y_early")
        y_late = [keep.tile([P, N], F32, name="y_late%d" % c) for c in range(EARLY, BLOCKS)]
        x_low = keep.tile([P, PACK * X_HALF], F32, name="x_low", align_bytes=64)
        x_high = shared.tile([P, PACK * X_HALF], F32, name="x_high", offset=2 * N, align_bytes=64)
        x_raw = [half[:].rearrange("p (t r) -> p t r", t=PACK) for half in (x_low, x_high)]

        nc.vector.memset(rows[:], 0.0)
        nc.sync.dma_start(y_early[:], y[0:EARLY * P, :].rearrange("(c p) n -> p c n", p=P))
        nc.sync.dma_start(rows[0:4, :], norm[0:1, :].rearrange("o (j m) -> (o j) m", m=P))
        nc.sync.dma_start(rows[4:8, :], ts[0:1, :].rearrange("o (j m) -> (o j) m", m=P))
        nc.sync.dma_start(rows[8:12, :], wt.rearrange("(j m) o -> j (m o)", m=P))
        nc.sync.dma_start(windows[0][:], cb_planes[0])
        nc.sync.dma_start(offsets[:], offs)
        for t in range(1, PACK):
            nc.sync.dma_start(windows[t][:], cb_planes[t])
        for half in range(2):
            nc.sync.dma_start(x_raw[half], x_rows[:, :, half * X_HALF:(half + 1) * X_HALF])
        for c in range(EARLY, BLOCKS):
            nc.sync.dma_start(y_late[c - EARLY][:], y[c * P:(c + 1) * P, :])

        ident = keep.tile([P, P], F32, name="ident")
        make_identity(nc, ident[:])
        ident_bf = keep.tile([P, P], BF16, name="ident_bf")
        nc.vector.tensor_copy(ident_bf[:], ident[:])
        turned = bank(2)
        nc.tensor.transpose(turned[:, 0:P], rows[:], ident[:])
        cols = keep.tile([P, 12], F32, name="cols")
        nc.vector.tensor_copy(cols[:], turned[:, 0:12])

        def spread(w, first):
            spread_bank = bank(w)
            for j in range(4):
                nc.tensor.transpose(spread_bank[:, j * P:(j + 1) * P],
                                    cols[:, first + j:first + j + 1].to_broadcast([P, P]), ident[:])
            return spread_bank

        norm_row = keep.tile([P, N], F32, name="norm_row")
        nc.scalar.copy(norm_row[:], spread(3, 0)[:])
        neg_ts = keep.tile([P, N], F32, name="neg_ts")
        nc.scalar.activation(dealt_in_words(neg_ts[:]), in_words(spread(4, 4)[:]), COPY, scale=-1.0)
        ts_sq = keep.tile([P, N], F32, name="ts_sq")
        nc.vector.tensor_tensor(ts_sq[:], neg_ts[:], neg_ts[:], MULT)
        ts_bank = bank(5)
        for s in range(PACK):
            nc.tensor.transpose(ts_bank[:, s * P:(s + 1) * P], neg_ts[:, s * P:(s + 1) * P], ident[:])
        neg_ts_words = keep.tile([P, P, PACK], F32, name="neg_ts_words")
        nc.scalar.copy(neg_ts_words[:], ts_bank[:].rearrange("m (s r) -> m r s", s=PACK))

        def wt_col(c):
            return cols[:, 8 + c:9 + c]

        k_bf = keep.tile([P, N, PACK], BF16, name="k_bf", align_bytes=64)
        k_codes = keep.tile([P, N], U32, name="k_codes", align_bytes=64)
        k_scales = keep.tile([P, N], U8, name="k_scales", align_bytes=64)
        kt_codes = keep.tile([P, D], U32, name="kt_codes", align_bytes=64)
        kt_scales = keep.tile([P, D], U8, name="kt_scales", align_bytes=64)
        k_dealt = k_bf[:].rearrange("p (s g i) t -> p g s i t", s=PACK, i=2)
        k_f32 = [keep.tile([P, N], F32, name="k_f32_%d" % t, align_bytes=64) for t in range(PACK)]
        kt_early = keep.tile([P, 2, 2, P // 2, PACK], BF16, name="kt_early", align_bytes=64)
        kt_late = shared.tile([P, 2, 2, P // 2, PACK], BF16, name="kt_late", offset=0, align_bytes=64)
        kt_pairs = [kt_early, kt_late]

        def gather(t):
            for j in range(CHUNKS):
                n_cols = slice(j * CHUNK, (j + 1) * CHUNK)
                picked = windows[t][:].indirect(offsets[:, j * LIST_COLS:(j + 1) * LIST_COLS])
                nc.vector.tensor_tensor(k_f32[t][:, n_cols], picked, norm_row[:, n_cols], MULT)
            for j in range(CHUNKS):
                src = k_f32[t][:, j * CHUNK:(j + 1) * CHUNK].rearrange("p (g i s) -> p g s i", i=2, s=PACK)
                dst = k_dealt[:, j * 16:(j + 1) * 16, :, :, t]
                if j < CHUNKS // 2:
                    nc.scalar.copy(dst, src)
                else:
                    nc.vector.tensor_copy(dst, src)

        def turn_k(t, w):
            kt_bank = bank(w, BF16)
            for s in range(PACK):
                nc.tensor.transpose(kt_bank[:, s * P:(s + 1) * P], k_bf[:, s * P:(s + 1) * P, t], ident_bf[:])
            return kt_bank

        def copy_kt(t, kt_bank):
            nc.scalar.copy(kt_pairs[t // 2][:, :, t % 2], kt_bank[:].rearrange("m (s h p) -> m h p s", s=PACK, h=2))

        def quantize_kt(pair):
            for half in range(2):
                place = 2 + pair if half else 1 - pair
                d_cols = slice(place * P, (place + 1) * P)
                nc.vector.quantize_mx(out=kt_codes[:, d_cols].bitcast(E4M3), scales=kt_scales[:, d_cols],
                                      in_=kt_pairs[pair][:, half].rearrange("m t p s -> m (t p s)"))

        h_banks = {}

        def turn_onto(c, term, first):
            for s in range(PACK):
                nc.tensor.matmul(h_banks[c][:, s * P:(s + 1) * P], term[:, s * P:(s + 1) * P], ident[:],
                                 start=(first and s == 0), stop=(not first and s == PACK - 1), is_transpose=True)

        y_weight = keep.tile([P, N], F32, name="y_weight")
        nc.scalar.activation(y_weight[:], neg_ts[:], COPY, scale=wt_col(3))
        s_weight = [keep.tile([P, N], F32, name="s_weight%d" % c) for c in range(BLOCKS)]
        for c in range(BLOCKS):
            factor = neg_ts if c == 2 else ts_sq
            nc.vector.tensor_scalar_mul(s_weight[c][:], factor[:], wt_col(c))
        weight_bank = bank(6)
        for s in range(PACK):
            nc.tensor.transpose(weight_bank[:, s * P:(s + 1) * P], s_weight[3][:, s * P:(s + 1) * P], ident[:])
        turned_weight = keep.tile([P, N], F32, name="turned_weight")
        nc.scalar.copy(turned_weight[:], weight_bank[:])
        for c in range(EARLY):
            y_term = keep.tile([P, N], F32, name="y_term%d" % c)
            nc.vector.scalar_tensor_tensor(dealt_in_words(y_term[:]), in_words(y_early[:, c, :]), wt_col(c),
                                           dealt_in_words(neg_ts[:]), MULT, MULT)
            h_banks[c] = bank(c)
            turn_onto(c, y_term, True)

        last = PACK - 1
        for t in range(2):
            gather(t)
            copy_kt(t, turn_k(t, 2 + t))
        quantize_kt(0)
        gather(2)
        held_kt_bank = turn_k(2, 7)
        gather(last)

        warm = bank(2)
        nc.tensor.transpose(warm[:, 0:P], k_f32[last][:, P:2 * P], ident[:])
        for i in range(4):
            nc.tensor.matmul_mx(out=warm[:, P:3 * P], lhsT=kt_codes[:, P:2 * P].bitcast(E4M3),
                                lhsT_scale=kt_scales[:, P:2 * P], rhs=kt_codes[:, P:3 * P].bitcast(E4M3),
                                rhs_scale=kt_scales[:, P:3 * P],
                                start=True, stop=True)
        last_kt_bank = turn_k(last, 3)

        x_pairs = [keep.tile([P, 2, P, PACK], BF16, name="x_pair%d" % half, tag="x_pair%d" % half, align_bytes=64)
                   for half in range(2)]
        x_codes = [keep.tile([P, P], U32, name="x_codes%d" % c, align_bytes=64) for c in range(BLOCKS)]
        x_scales = [keep.tile([P, P], U8, name="x_scales%d" % c, align_bytes=64) for c in range(BLOCKS)]

        def interleave_x(c, copy):
            r_cols = slice((c % 2) * P, (c % 2 + 1) * P)
            copy(x_pairs[c // 2][:, c % 2].rearrange("p (g i) t -> p g t i", i=4),
                 x_raw[c // 2][:, :, r_cols].rearrange("p t (g i) -> p g t i", i=4))

        def quantize_x(c):
            nc.vector.quantize_mx(out=x_codes[c][:].bitcast(E4M3), scales=x_scales[c][:],
                                  in_=x_pairs[c // 2][:, c % 2].rearrange("p r t -> p (r t)"))

        interleave_x(0, nc.scalar.copy)
        interleave_x(1, nc.scalar.copy)
        interleave_x(3, nc.scalar.copy)
        for half in range(2):
            for s in range(PACK):
                n_cols = slice(s * P + half * P // 2, s * P + (half + 1) * P // 2)
                nc.vector.quantize_mx(out=k_codes[:, n_cols].bitcast(E4M3), scales=k_scales[:, n_cols],
                                      in_=k_bf[:, n_cols, :].rearrange("p n t -> p (n t)"))
        quantize_x(0)
        quantize_x(1)
        interleave_x(2, nc.vector.tensor_copy)
        y_term2 = keep.tile([P, N], F32, name="y_term2")
        nc.scalar.activation(dealt_in_words(y_term2[:]), in_words(y_late[0][:]), COPY, scale=wt_col(2))
        copy_kt(last, last_kt_bank)
        copy_kt(2, held_kt_bank)
        quantize_x(3)
        quantize_x(2)

        s_banks = {}
        for c, w in enumerate((2, 4, 5)):
            s_banks[c] = bank(w)
            nc.tensor.matmul_mx(out=s_banks[c][:], lhsT=x_codes[c][:].bitcast(E4M3), lhsT_scale=x_scales[c][:],
                                rhs=k_codes[:].bitcast(E4M3), rhs_scale=k_scales[:], start=True, stop=True)
        s_banks[3] = bank(6)
        for s in range(PACK):
            n_cols = slice(s * P, (s + 1) * P)
            nc.tensor.matmul_mx(out=s_banks[3][:, n_cols], lhsT=k_codes[:, n_cols].bitcast(E4M3),
                                lhsT_scale=k_scales[:, n_cols], rhs=x_codes[3][:].bitcast(E4M3),
                                rhs_scale=x_scales[3][:], start=True, stop=True)

        y_term3 = keep.tile([P, N], F32, name="y_term3", tag="x_pair1", align_bytes=64)
        nc.gpsimd.tensor_tensor(y_term3[:].rearrange("p (s m) -> p s m", s=PACK),
                                y_late[1][:].rearrange("p (m s) -> p s m", s=PACK),
                                y_weight[:].rearrange("p (s m) -> p s m", s=PACK), MULT)

        a_term2 = keep.tile([P, N], F32, name="a_term2")
        a_term3 = keep.tile([P, N], F32, name="a_term3")
        a_term0 = shared.tile([P, N], F32, name="a_term0", offset=4 * N, align_bytes=64)
        a_term1 = shared.tile([P, N], F32, name="a_term1", offset=8 * N, align_bytes=64)
        a_terms = [a_term0[:], a_term1[:], a_term2[:], a_term3[:]]
        for c in range(BLOCKS):
            weight = s_weight[c] if c < 3 else turned_weight
            nc.vector.tensor_tensor(a_terms[c], s_banks[c][:], weight[:], MULT)

        for c in range(EARLY):
            turn_onto(c, a_terms[c], False)
        h_banks[3] = bank(3)
        for s in range(PACK):
            nc.tensor.transpose(h_banks[3][:, s * P:(s + 1) * P], y_term3[:, s * P:(s + 1) * P], ident[:])
        h_banks[2] = bank(5)
        turn_onto(2, y_term2, True)
        turn_onto(2, a_terms[2], False)

        h_bf = [keep.tile([P, P, PACK], BF16, name="h_bf%d" % c, align_bytes=64) for c in range(BLOCKS)]
        h_scales = [keep.tile([P, P], U8, name="h_scales%d" % c, align_bytes=64) for c in range(BLOCKS)]
        h_codes = {}
        o_banks = {}

        def h_words(c):
            return h_banks[c][:].rearrange("m (s r) -> m r s", s=PACK)

        def quantize_h(c, tag):
            h_codes[c] = keep.tile([P, P], U32, name="h_codes%d" % c, tag=tag, align_bytes=64)
            nc.vector.quantize_mx(out=h_codes[c][:].bitcast(E5M2), scales=h_scales[c][:],
                                  in_=h_bf[c][:].rearrange("m r s -> m (r s)"))

        def second_product(c, banks):
            for half, w in enumerate(banks):
                d_cols = slice(half * D_HALF, (half + 1) * D_HALF)
                o_banks[c, half] = bank(w)
                nc.tensor.matmul_mx(out=o_banks[c, half][:, 0:D_HALF], lhsT=h_codes[c][:].bitcast(E5M2),
                                    lhsT_scale=h_scales[c][:], rhs=kt_codes[:, d_cols].bitcast(E4M3),
                                    rhs_scale=kt_scales[:, d_cols], start=True, stop=True)

        def store(c, copies):
            result = keep.tile([P, P, PACK], F32, name="result%d" % c, align_bytes=64)
            for half, copy in enumerate(copies):
                by_pair = o_banks[c, half][:, 0:D_HALF].rearrange("r (u e p) -> r p u e", u=2, e=2)
                copy(result[:, half * P // 2:(half + 1) * P // 2, :].rearrange("r p (u e) -> r p u e", e=2),
                     by_pair if half else by_pair[:, :, ::-1, :])
            nc.sync.dma_start(out[c * P:(c + 1) * P, :], result[:].rearrange("r p t -> r (p t)"))

        for c in range(EARLY):
            nc.scalar.copy(h_bf[c][:], h_words(c))
        quantize_kt(1)
        quantize_h(0, "h_codes0")
        nc.vector.tensor_tensor(h_bf[3][:].rearrange("m (g i) s -> m g s i", i=4),
                                a_terms[3].rearrange("m (s g i) -> m g s i", s=PACK, i=4),
                                h_banks[3][:].rearrange("m (s g i) -> m g s i", s=PACK, i=4), ADD)
        quantize_h(1, "h_codes1")
        nc.vector.tensor_tensor(h_bf[2][:], h_words(2), neg_ts_words[:], MULT)
        quantize_h(3, "h_codes3")
        quantize_h(2, "h_codes2")
        for c, banks in ((0, (2, 4)), (1, (6, 7)), (3, (0, 1)), (2, (3, 5))):
            second_product(c, banks)
        store(0, (nc.scalar.copy, nc.scalar.copy))
        for c in (1, 3, 2):
            store(c, (nc.scalar.copy, nc.vector.tensor_copy))
